import numpy as np
import ml_dtypes


def mxq(x, axis, fmt="e4m3"):
    dtype, down = {"e4m3": (ml_dtypes.float8_e4m3fn, 7), "e5m2": (ml_dtypes.float8_e5m2, 14)}[fmt]
    v = np.moveaxis(np.asarray(x, np.float32).astype(ml_dtypes.bfloat16).astype(np.float64), axis, -1)
    blocks = v.reshape(v.shape[:-1] + (-1, 32))
    amax = np.abs(blocks).max(-1, keepdims=True)
    byte = np.maximum(np.where(amax > 0, np.frexp(amax)[1] - 1 + 127, 0) - down, 1)
    scale = np.exp2(byte - 127.0)
    codes = (blocks / scale).astype(np.float32).astype(dtype).astype(np.float64)
    return np.moveaxis((codes * scale).reshape(v.shape), -1, axis)


WIDE = False


def mx_kscale(k):
    if not WIDE:
        return np.ones(k)
    levels = np.array([10, -10, 5, -5, 0])
    if k % 512:
        return np.exp2(np.random.permutation(np.resize(levels, k // 32))).repeat(32)
    a = np.empty((k // 512, 16))
    for p in range(k // 512):
        a[p, :8] = np.random.permutation(np.resize(levels, 8))
        for g in range(8):
            far = levels[np.abs(levels - a[p, g]) >= 10]
            a[p, g + 8] = far[np.random.randint(len(far))]
    return np.exp2(a.ravel()).repeat(32)


def f64(x):
    return np.asarray(x).astype(np.float64)


def striped(idx):
    return np.tile(idx.reshape(-1, 16).T, (8, 1)).astype(np.uint16)


def unstriped(offs):
    return offs[:16].T.reshape(-1).astype(np.int64)

def planes(y):
    n, m = y.shape
    v = y.astype(np.float32).astype(ml_dtypes.bfloat16).astype(np.float64).reshape(n // 32, 32, m)
    top = np.abs(v).max(1)
    byte = np.clip(np.where(top > 0, np.frexp(top)[1] - 1 + 127 - 7, 1), 1, 254)
    codes = (v * np.exp2(127.0 - byte)[:, None, :]).reshape(n, m).astype(np.float32).astype(ml_dtypes.float8_e4m3fn).view(np.uint8)
    words = codes.reshape(n // 512, 128, 4, m).transpose(0, 1, 3, 2)
    return np.ascontiguousarray(words), np.ascontiguousarray(byte.astype(np.uint8).reshape(n // 512, 16, m))


K, T, S, H = 512, 1024, 512, 512
P = 2 ** 7


def setup_inputs():
    n = np.random.standard_normal
    s = mx_kscale(K)[:, None]
    u = mx_kscale(H)
    return {
        "xT": (n((K, T)) * s).astype(np.float32),
        "w1": (n((K, H)) / np.sqrt(K) / s * u).astype(np.float32),
        "w2": (n((H, H)) / np.sqrt(H) / u[:, None]).astype(np.float32),
        "lam": np.tile(np.random.uniform(0.1, 0.9, S), (P, 1)).astype(np.float32),
        "mu": np.tile(np.random.uniform(0.1, 0.9, S), (P, 1)).astype(np.float32),
        "offs": striped(np.random.permutation(T)[:S]),
        "pos1": striped(np.random.permutation(S)),
    }


def reference(xT, w1, w2, lam, mu, offs, pos1):
    xq = mxq(f64(xT)[:, unstriped(offs)], 0, "e4m3")
    h = mxq(f64(w1), 0, "e4m3").T @ xq
    z = h * f64(lam)[:1] + h[:, unstriped(pos1)] * f64(mu)[:1]
    out_0 = mxq(f64(w2), 0, "e4m3").T @ mxq(z, 0, "e4m3")
    return (out_0,) + planes(out_0)

@@ -1,0 +1,206 @@
+from contextlib import ExitStack
+
+import concourse.mybir as mybir
+
+K, T, S, H = 512, 1024, 512, 512
+FLOPS = 2 * K * H * S + 2 * H * H * S
+
+F32 = mybir.dt.float32
+BF16 = mybir.dt.bfloat16
+I32 = mybir.dt.int32
+U32 = mybir.dt.uint32
+U16 = mybir.dt.uint16
+U8 = mybir.dt.uint8
+FP8X4 = mybir.dt.float8_e4m3fn_x4
+MULT = mybir.AluOpType.mult
+ADD = mybir.AluOpType.add
+
+P = 128
+PACK = 4
+RUN = 4
+CHUNKS = ((0, 256), (256, 128), (384, 128))
+
+
+def tile_picked_mixup_none_lo_kernel(tc, xT, w1, w2, lam, mu, offs, pos1, out_0, out_1, out_2):
+    nc = tc.nc
+    with ExitStack() as ctx:
+        keep = ctx.enter_context(tc.tile_pool(name="keep", bufs=1))
+        psum = ctx.enter_context(tc.psum_pool(name="psum", bufs=1))
+
+        offs_sb = keep.tile([P, S // 16], U16, name="offs_sb")
+        pos_sb = keep.tile([P, S // 16], U16, name="pos_sb")
+        x_rows = xT.rearrange("(p t) n -> p t n", t=PACK)
+        w1_rows = w1.rearrange("(p j) c -> p j c", j=PACK)
+        w2_rows = w2.rearrange("(p j) c -> p j c", j=PACK)
+
+        x_plane = [keep.tile([P, T], F32, name=f"x_plane{t}") for t in range(PACK)]
+        w1_half = [keep.tile([P, PACK, H // 2], F32, name=f"w1_half{u}") for u in range(2)]
+        w2_raw = keep.tile([P, PACK, H], F32, name="w2_raw")
+        lam_sb = keep.tile([P, S], F32, name="lam_sb")
+        mu_sb = keep.tile([P, S], F32, name="mu_sb")
+
+        nc.sync.dma_start(x_plane[0][:], x_rows[:, 0, :])
+        nc.sync.dma_start(offs_sb[:], offs)
+        for t in range(1, PACK):
+            nc.sync.dma_start(x_plane[t][:], x_rows[:, t, :])
+        for u in range(2):
+            nc.sync.dma_start(w1_half[u][:], w1_rows[:, :, u * (H // 2) : (u + 1) * (H // 2)])
+        nc.sync.dma_start(lam_sb[:], lam)
+        nc.sync.dma_start(mu_sb[:], mu)
+        nc.sync.dma_start(pos_sb[:], pos1)
+        nc.sync.dma_start(w2_raw[:], w2_rows)
+
+        x_pair = [keep.tile([P, 2, S], F32, name=f"x_pair{u}") for u in range(2)]
+        x_bf = keep.tile([P, S, PACK], BF16, name="x_bf", align_bytes=64)
+        x_codes = keep.tile([P, S], U32, name="x_codes", align_bytes=64)
+        x_scales = keep.tile([P, S], U8, name="x_scales", align_bytes=64)
+        w1_bf = keep.tile([P, PACK, P, PACK], BF16, name="w1_bf", align_bytes=64)
+        w1_codes = keep.tile([P, H], U32, name="w1_codes", align_bytes=64)
+        w1_scales = keep.tile([P, H], U8, name="w1_scales", align_bytes=64)
+
+        def gather_x(t):
+            nc.vector.tensor_copy(x_pair[t // 2][:, t % 2, :], x_plane[t][:].indirect(offs_sb[:]))
+
+        gather_x(0)
+        gather_x(1)
+        nc.scalar.copy(x_bf[:, :, 0:2], x_pair[0][:].rearrange("p e n -> p n e"))
+        gather_x(2)
+        gather_x(3)
+        nc.vector.tensor_copy(x_bf[:, :, 2:4], x_pair[1][:].rearrange("p e n -> p n e"))
+        for u in range(2):
+            nc.scalar.copy(
+                w1_bf[:, :, u * (P // 2) : (u + 1) * (P // 2), :].rearrange("p t m j -> p m j t"),
+                w1_half[u][:].rearrange("p j (m t) -> p m j t", t=PACK),
+            )
+        nc.vector.quantize_mx(x_codes[:].bitcast(FP8X4), x_scales[:], x_bf[:].rearrange("p n t -> p (n t)"))
+
+        h_ps = [psum.tile([P, S], F32, name=f"h_ps{t}") for t in range(PACK)]
+        h_sb = [keep.tile([P, S], F32, name=f"h_sb{t}") for t in range(PACK)]
+        own = keep.tile([P, PACK, S], F32, name="own")
+        for t in range(PACK):
+            cols = slice(P * t, P * (t + 1))
+            nc.vector.quantize_mx(w1_codes[:, cols].bitcast(FP8X4), w1_scales[:, cols], w1_bf[:, t, :, :].rearrange("p m j -> p (m j)"))
+            nc.tensor.matmul_mx(
+                out=h_ps[t][:],
+                lhsT=w1_codes[:, cols].bitcast(FP8X4),
+                lhsT_scale=w1_scales[:, cols],
+                rhs=x_codes[:].bitcast(FP8X4),
+                rhs_scale=x_scales[:],
+                start=True,
+                stop=True,
+            )
+
+        def own_share(t):
+            nc.vector.tensor_tensor(own[:, t, :], h_ps[t][:], lam_sb[:], MULT)
+
+        def window(t):
+            nc.scalar.copy(h_sb[t][:], h_ps[t][:])
+
+        partner = [keep.tile([P, PACK, CHUNKS[0][1]], F32, name="partner0")]
+
+        def gather_h(c, t):
+            j0, n = CHUNKS[c]
+            nc.vector.tensor_tensor(partner[c][:, t, :], h_sb[t][:].indirect(pos_sb[:, j0 // 16 : (j0 + n) // 16]), mu_sb[:, j0 : j0 + n], MULT)
+
+        own_share(0)
+        window(0)
+        own_share(1)
+        window(1)
+        gather_h(0, 0)
+        window(2)
+        gather_h(0, 1)
+        window(3)
+        own_share(2)
+        gather_h(0, 2)
+        own_share(3)
+        gather_h(0, 3)
+
+        w2_bf = keep.tile([P, PACK, P, PACK], BF16, name="w2_bf", tag="late", align_bytes=64)
+        w2_codes = keep.tile([P, H], U32, name="w2_codes", align_bytes=64)
+        w2_scales = keep.tile([P, H], U8, name="w2_scales", align_bytes=64)
+        nc.scalar.copy(
+            w2_bf[:].rearrange("p t m j -> p m j t"),
+            w2_raw[:].rearrange("p j (m t) -> p m j t", t=PACK),
+        )
+
+        y_rows = out_0.rearrange("(p t) n -> p t n", t=PACK)
+        y_words = out_1.rearrange("z p c r -> p (z c r)").bitcast(I32)
+        y_scale_rows = out_2.rearrange("z q c -> q (z c)").bitcast(I32)
+        y_scales = keep.tile([P, S], U8, name="y_scales", align_bytes=64)
+
+        z_bf, z_codes, z_scales, y_sb, y_bf, y_codes, y_ps = [], [], [], [], [], [], []
+        for c, (j0, n) in enumerate(CHUNKS):
+            z_bf.append(keep.tile([P, n, PACK], BF16, name=f"z_bf{c}", align_bytes=64))
+            z_codes.append(keep.tile([P, n], U32, name=f"z_codes{c}", align_bytes=64))
+            z_scales.append(keep.tile([P, n], U8, name=f"z_scales{c}", align_bytes=64))
+            y_sb.append(keep.tile([P, PACK, n], F32, name=f"y_sb{c}"))
+            y_bf.append(keep.tile([P, n, PACK], BF16, name=f"y_bf{c}", align_bytes=64))
+            y_codes.append(keep.tile([P, n], U32, name=f"y_codes{c}", align_bytes=64))
+
+        def mix(c):
+            j0, n = CHUNKS[c]
+            nc.vector.tensor_tensor(
+                z_bf[c][:].rearrange("p (g i) t -> p g t i", i=RUN),
+                own[:, :, j0 : j0 + n].rearrange("p t (g i) -> p g t i", i=RUN),
+                partner[c][:, :, :].rearrange("p t (g i) -> p g t i", i=RUN),
+                ADD,
+            )
+
+        def quantise_z(c):
+            nc.vector.quantize_mx(z_codes[c][:].bitcast(FP8X4), z_scales[c][:], z_bf[c][:].rearrange("p n t -> p (n t)"))
+
+        def second_layer(c):
+            j0, n = CHUNKS[c]
+            for u in range(2):
+                bank = psum.tile([P, 2, n], F32, name=f"y_ps{c}_{u}", tag=f"y_ps{c % 2}_{u}")
+                for e in range(2):
+                    cols = slice(P * (2 * u + e), P * (2 * u + e + 1))
+                    nc.tensor.matmul_mx(
+                        out=bank[:, e, :],
+                        lhsT=w2_codes[:, cols].bitcast(FP8X4),
+                        lhsT_scale=w2_scales[:, cols],
+                        rhs=z_codes[c][:].bitcast(FP8X4),
+                        rhs_scale=z_scales[c][:],
+                        start=True,
+                        stop=True,
+                    )
+                nc.scalar.copy(y_sb[c][:, 2 * u : 2 * u + 2, :], bank[:])
+            nc.sync.dma_start(y_rows[:, :, j0 : j0 + n], y_sb[c][:])
+
+        def round_y(c, copy):
+            copy(
+                y_bf[c][:].rearrange("p (g i) t -> p g t i", i=RUN),
+                y_sb[c][:].rearrange("p t (g i) -> p g t i", i=RUN),
+            )
+
+        def quantise_y(c):
+            j0, n = CHUNKS[c]
+            nc.vector.quantize_mx(y_codes[c][:].bitcast(FP8X4), y_scales[:, j0 : j0 + n], y_bf[c][:].rearrange("p n t -> p (n t)"))
+            nc.sync.dma_start(y_words[:, j0 : j0 + n], y_codes[c][:].bitcast(I32))
+
+        mix(0)
+        nc.vector.quantize_mx(w2_codes[:].bitcast(FP8X4), w2_scales[:], w2_bf[:].rearrange("p t m j -> p (t m j)"))
+        quantise_z(0)
+        second_layer(0)
+        round_y(0, nc.scalar.copy)
+        late = keep.tile([P, 2, PACK, CHUNKS[1][1]], F32, name="partner_late", tag="late", align_bytes=64)
+        partner.extend([late[:, 0, :, :], late[:, 1, :, :]])
+        for t in range(PACK):
+            gather_h(1, t)
+        mix(1)
+        gather_h(2, 0)
+        quantise_z(1)
+        second_layer(1)
+        round_y(1, nc.scalar.copy)
+        for t in range(1, PACK):
+            gather_h(2, t)
+        mix(2)
+        quantise_y(0)
+        quantise_z(2)
+        second_layer(2)
+        quantise_y(1)
+        round_y(2, nc.vector.tensor_copy)
+        quantise_y(2)
+        for q in range(4):
+            queue = nc.sync if q % 2 == 0 else nc.scalar
+            queue.dma_start(y_scale_rows[4 * q : 4 * q + 4, :], y_scales[32 * q : 32 * q + 4, :].bitcast(I32))

@@ -1,6 +1,7 @@
 from contextlib import ExitStack
 
 import concourse.mybir as mybir
+from concourse.masks import make_identity
 
 K, T, S, H = 512, 1024, 512, 512
 FLOPS = 2 * K * H * S + 2 * H * H * S
@@ -14,11 +15,16 @@ U8 = mybir.dt.uint8
 FP8X4 = mybir.dt.float8_e4m3fn_x4
 MULT = mybir.AluOpType.mult
 ADD = mybir.AluOpType.add
+COPY = mybir.ActivationFunctionType.Copy
 
 P = 128
 PACK = 4
-RUN = 4
+RUN = 2
+HALF = S // 2
 CHUNKS = ((0, 256), (256, 128), (384, 128))
+GATHERS = ((0, 384), (384, 128))
+W1_SPLIT = 104
+W2_SPLIT = 44
 
 
 def tile_picked_mixup_none_lo_kernel(tc, xT, w1, w2, lam, mu, offs, pos1, out_0, out_1, out_2):
@@ -34,21 +40,33 @@ def tile_picked_mixup_none_lo_kernel(tc, xT, w1, w2, lam, mu, offs, pos1, out_0,
         w2_rows = w2.rearrange("(p j) c -> p j c", j=PACK)
 
         x_plane = [keep.tile([P, T], F32, name=f"x_plane{t}") for t in range(PACK)]
-        w1_half = [keep.tile([P, PACK, H // 2], F32, name=f"w1_half{u}") for u in range(2)]
-        w2_raw = keep.tile([P, PACK, H], F32, name="w2_raw")
-        lam_sb = keep.tile([P, S], F32, name="lam_sb")
-        mu_sb = keep.tile([P, S], F32, name="mu_sb")
+        w1_half = [keep.tile([P, PACK, HALF], F32, name=f"w1_half{u}") for u in range(2)]
+        w2_half = [keep.tile([P, PACK, HALF], F32, name=f"w2_half{u}") for u in range(2)]
+        lam_rows = keep.tile([P, P], F32, name="lam_rows")
+        mu_part = [keep.tile([P, n], F32, name=f"mu_part{g}") for g, (j0, n) in enumerate(GATHERS)]
+        identity = keep.tile([P, P], F32, name="identity")
+        make_identity(nc, identity[:])
 
         nc.sync.dma_start(x_plane[0][:], x_rows[:, 0, :])
         nc.sync.dma_start(offs_sb[:], offs)
         for t in range(1, PACK):
             nc.sync.dma_start(x_plane[t][:], x_rows[:, t, :])
         for u in range(2):
-            nc.sync.dma_start(w1_half[u][:], w1_rows[:, :, u * (H // 2) : (u + 1) * (H // 2)])
-        nc.sync.dma_start(lam_sb[:], lam)
-        nc.sync.dma_start(mu_sb[:], mu)
+            nc.sync.dma_start(w1_half[u][:], w1_rows[:, :, u * HALF : (u + 1) * HALF])
+        nc.sync.dma_start(w2_half[0][:], w2_rows[:, :, 0:HALF])
+        nc.sync.dma_start(lam_rows[:], lam.rearrange("r (b m) -> (r b) m", m=P)[0:P, :])
+        nc.sync.dma_start(mu_part[0][:], mu[:, 0 : GATHERS[0][1]])
         nc.sync.dma_start(pos_sb[:], pos1)
-        nc.sync.dma_start(w2_raw[:], w2_rows)
+        nc.sync.dma_start(w2_half[1][:], w2_rows[:, :, HALF:S])
+        nc.sync.dma_start(mu_part[1][:], mu[:, GATHERS[1][0] : S])
+
+        def deal(copy, dst, src, m0, m1):
+            u = m0 // (P // 2)
+            base = u * (P // 2)
+            copy(
+                dst[:, :, m0:m1, :].rearrange("p t m j -> p m j t"),
+                src[u][:, :, PACK * (m0 - base) : PACK * (m1 - base)].rearrange("p j (m t) -> p m j t", t=PACK),
+            )
 
         x_pair = [keep.tile([P, 2, S], F32, name=f"x_pair{u}") for u in range(2)]
         x_bf = keep.tile([P, S, PACK], BF16, name="x_bf", align_bytes=64)
@@ -57,78 +75,114 @@ def tile_picked_mixup_none_lo_kernel(tc, xT, w1, w2, lam, mu, offs, pos1, out_0,
         w1_bf = keep.tile([P, PACK, P, PACK], BF16, name="w1_bf", align_bytes=64)
         w1_codes = keep.tile([P, H], U32, name="w1_codes", align_bytes=64)
         w1_scales = keep.tile([P, H], U8, name="w1_scales", align_bytes=64)
+        w2_bf = keep.tile([P, PACK, P, PACK], BF16, name="w2_bf", align_bytes=64)
+        w2_codes = keep.tile([P, H], U32, name="w2_codes", align_bytes=64)
+        w2_scales = keep.tile([P, H], U8, name="w2_scales", align_bytes=64)
+        halves = [slice(0, HALF), slice(HALF, S)]
 
-        def gather_x(t):
-            nc.vector.tensor_copy(x_pair[t // 2][:, t % 2, :], x_plane[t][:].indirect(offs_sb[:]))
+        def gather_x(t, j0, j1):
+            nc.vector.tensor_copy(x_pair[t // 2][:, t % 2, j0:j1], x_plane[t][:].indirect(offs_sb[:, j0 // 16 : j1 // 16]))
 
-        gather_x(0)
-        gather_x(1)
+        gather_x(0, 0, S)
+        gather_x(1, 0, S)
         nc.scalar.copy(x_bf[:, :, 0:2], x_pair[0][:].rearrange("p e n -> p n e"))
-        gather_x(2)
-        gather_x(3)
-        nc.vector.tensor_copy(x_bf[:, :, 2:4], x_pair[1][:].rearrange("p e n -> p n e"))
-        for u in range(2):
-            nc.scalar.copy(
-                w1_bf[:, :, u * (P // 2) : (u + 1) * (P // 2), :].rearrange("p t m j -> p m j t"),
-                w1_half[u][:].rearrange("p j (m t) -> p m j t", t=PACK),
-            )
-        nc.vector.quantize_mx(x_codes[:].bitcast(FP8X4), x_scales[:], x_bf[:].rearrange("p n t -> p (n t)"))
+        gather_x(2, 0, S)
+        gather_x(3, 0, HALF)
+        gather_x(3, HALF, S)
+        for half in halves:
+            nc.vector.tensor_copy(x_bf[:, half, 2:4], x_pair[1][:, :, half].rearrange("p e n -> p n e"))
+        deal(nc.scalar.copy, w1_bf, w1_half, 0, P // 2)
+        for half in halves:
+            nc.vector.quantize_mx(x_codes[:, half].bitcast(FP8X4), x_scales[:, half], x_bf[:, half, :].rearrange("p n t -> p (n t)"))
+        deal(nc.scalar.copy, w1_bf, w1_half, P // 2, W1_SPLIT)
+        deal(nc.vector.tensor_copy, w1_bf, w1_half, W1_SPLIT, P)
+        deal(nc.scalar.copy, w2_bf, w2_half, 0, W2_SPLIT)
 
-        h_ps = [psum.tile([P, S], F32, name=f"h_ps{t}") for t in range(PACK)]
         h_sb = [keep.tile([P, S], F32, name=f"h_sb{t}") for t in range(PACK)]
-        own = keep.tile([P, PACK, S], F32, name="own")
-        for t in range(PACK):
+
+        def first_layer(t, cols_j, tag):
             cols = slice(P * t, P * (t + 1))
-            nc.vector.quantize_mx(w1_codes[:, cols].bitcast(FP8X4), w1_scales[:, cols], w1_bf[:, t, :, :].rearrange("p m j -> p (m j)"))
+            h_ps = psum.tile([P, cols_j.stop - cols_j.start], F32, name=f"h_ps_{tag}", tag=tag)
             nc.tensor.matmul_mx(
-                out=h_ps[t][:],
+                out=h_ps[:],
                 lhsT=w1_codes[:, cols].bitcast(FP8X4),
                 lhsT_scale=w1_scales[:, cols],
-                rhs=x_codes[:].bitcast(FP8X4),
-                rhs_scale=x_scales[:],
+                rhs=x_codes[:, cols_j].bitcast(FP8X4),
+                rhs_scale=x_scales[:, cols_j],
                 start=True,
                 stop=True,
             )
+            return h_ps
 
-        def own_share(t):
-            nc.vector.tensor_tensor(own[:, t, :], h_ps[t][:], lam_sb[:], MULT)
+        h_banks = []
+        for t in range(PACK):
+            cols = slice(P * t, P * (t + 1))
+            nc.vector.quantize_mx(w1_codes[:, cols].bitcast(FP8X4), w1_scales[:, cols], w1_bf[:, t, :, :].rearrange("p m j -> p (m j)"))
+            if t == 0:
+                for u, half in enumerate(halves):
+                    h_banks.append((t, half, first_layer(t, half, f"bank{u}")))
+            else:
+                h_banks.append((t, slice(0, S), first_layer(t, slice(0, S), f"bank{t + 1}")))
 
-        def window(t):
-            nc.scalar.copy(h_sb[t][:], h_ps[t][:])
+        lam_ps = psum.tile([P, P], F32, name="lam_ps", tag="bank7")
+        lam_col = keep.tile([P, PACK], F32, name="lam_col")
+        nc.tensor.transpose(lam_ps[:], lam_rows[:], identity[:])
+        nc.scalar.copy(lam_col[:], lam_ps[:, 0:PACK])
 
-        partner = [keep.tile([P, PACK, CHUNKS[0][1]], F32, name="partner0")]
+        deal(nc.vector.tensor_copy, w2_bf, w2_half, W2_SPLIT, P // 2)
+        deal(nc.vector.tensor_copy, w2_bf, w2_half, P // 2, P)
+
+        for t, cols_j, h_ps in h_banks:
+            nc.scalar.copy(h_sb[t][:, cols_j], h_ps[:])
+
+        partner = [keep.tile([P, PACK, GATHERS[0][1]], F32, name="partner0", tag="partner")]
 
         def gather_h(c, t):
-            j0, n = CHUNKS[c]
-            nc.vector.tensor_tensor(partner[c][:, t, :], h_sb[t][:].indirect(pos_sb[:, j0 // 16 : (j0 + n) // 16]), mu_sb[:, j0 : j0 + n], MULT)
+            j0, n = GATHERS[c]
+            nc.vector.tensor_tensor(
+                partner[c][:, t, :],
+                h_sb[t][:].indirect(pos_sb[:, j0 // 16 : (j0 + n) // 16]),
+                mu_part[c][:],
+                MULT,
+            )
 
-        own_share(0)
-        window(0)
-        own_share(1)
-        window(1)
         gather_h(0, 0)
-        window(2)
-        gather_h(0, 1)
-        window(3)
-        own_share(2)
-        gather_h(0, 2)
-        own_share(3)
-        gather_h(0, 3)
+        nc.vector.quantize_mx(w2_codes[:].bitcast(FP8X4), w2_scales[:], w2_bf[:].rearrange("p t m j -> p (t m j)"))
+        for t in range(1, PACK):
+            gather_h(0, t)
 
-        w2_bf = keep.tile([P, PACK, P, PACK], BF16, name="w2_bf", tag="late", align_bytes=64)
-        w2_codes = keep.tile([P, H], U32, name="w2_codes", align_bytes=64)
-        w2_scales = keep.tile([P, H], U8, name="w2_scales", align_bytes=64)
-        nc.scalar.copy(
-            w2_bf[:].rearrange("p t m j -> p m j t"),
-            w2_raw[:].rearrange("p j (m t) -> p m j t", t=PACK),
-        )
+        turned_tags = ["bank5", "bank6", "bank0", "bank1"]
+        own_tags = ["bank2", "bank3", "bank4", "bank7"]
+        own_ps = []
+
+        def turn(b):
+            turned = psum.tile([P, PACK, P], F32, name=f"turned{b}", tag=turned_tags[b])
+            for t in range(PACK):
+                nc.tensor.transpose(turned[:, t, :], h_sb[t][:, P * b : P * (b + 1)], identity[:])
+            return turned
+
+        def scale_and_turn_back(b, turned):
+            scaled = keep.tile([P, PACK, P], F32, name=f"scaled{b}")
+            nc.scalar.activation(scaled[:], turned[:], COPY, scale=lam_col[:, b : b + 1])
+            own = psum.tile([P, PACK, P], F32, name=f"own{b}", tag=own_tags[b])
+            for t in range(PACK):
+                nc.tensor.transpose(own[:, t, :], scaled[:, t, :], identity[:])
+            own_ps.append(own)
+
+        turned = [turn(0), turn(1)]
+        scale_and_turn_back(0, turned[0])
+        turned.append(turn(2))
+        scale_and_turn_back(1, turned[1])
+        turned.append(turn(3))
+        scale_and_turn_back(2, turned[2])
+        scale_and_turn_back(3, turned[3])
 
         y_rows = out_0.rearrange("(p t) n -> p t n", t=PACK)
         y_words = out_1.rearrange("z p c r -> p (z c r)").bitcast(I32)
         y_scale_rows = out_2.rearrange("z q c -> q (z c)").bitcast(I32)
         y_scales = keep.tile([P, S], U8, name="y_scales", align_bytes=64)
 
-        z_bf, z_codes, z_scales, y_sb, y_bf, y_codes, y_ps = [], [], [], [], [], [], []
+        z_bf, z_codes, z_scales, y_sb, y_bf, y_codes = [], [], [], [], [], []
         for c, (j0, n) in enumerate(CHUNKS):
             z_bf.append(keep.tile([P, n, PACK], BF16, name=f"z_bf{c}", align_bytes=64))
             z_codes.append(keep.tile([P, n], U32, name=f"z_codes{c}", align_bytes=64))
@@ -137,22 +191,26 @@ def tile_picked_mixup_none_lo_kernel(tc, xT, w1, w2, lam, mu, offs, pos1, out_0,
             y_bf.append(keep.tile([P, n, PACK], BF16, name=f"y_bf{c}", align_bytes=64))
             y_codes.append(keep.tile([P, n], U32, name=f"y_codes{c}", align_bytes=64))
 
-        def mix(c):
-            j0, n = CHUNKS[c]
+        def mix(c, b):
+            j0 = P * b - CHUNKS[c][0]
+            g = b // 3
+            g0 = P * b - GATHERS[g][0]
             nc.vector.tensor_tensor(
-                z_bf[c][:].rearrange("p (g i) t -> p g t i", i=RUN),
-                own[:, :, j0 : j0 + n].rearrange("p t (g i) -> p g t i", i=RUN),
-                partner[c][:, :, :].rearrange("p t (g i) -> p g t i", i=RUN),
+                z_bf[c][:, j0 : j0 + P, :].rearrange("p (g i) t -> p g t i", i=RUN),
+                own_ps[b][:].rearrange("p t (g i) -> p g t i", i=RUN),
+                partner[g][:, :, g0 : g0 + P].rearrange("p t (g i) -> p g t i", i=RUN),
                 ADD,
             )
 
         def quantise_z(c):
             nc.vector.quantize_mx(z_codes[c][:].bitcast(FP8X4), z_scales[c][:], z_bf[c][:].rearrange("p n t -> p (n t)"))
 
+        y_tags = [["bank5", "bank6"], ["bank0", "bank1"], ["bank2", "bank3"]]
+
         def second_layer(c):
             j0, n = CHUNKS[c]
             for u in range(2):
-                bank = psum.tile([P, 2, n], F32, name=f"y_ps{c}_{u}", tag=f"y_ps{c % 2}_{u}")
+                bank = psum.tile([P, 2, n], F32, name=f"y_ps{c}_{u}", tag=y_tags[c][u])
                 for e in range(2):
                     cols = slice(P * (2 * u + e), P * (2 * u + e + 1))
                     nc.tensor.matmul_mx(
@@ -178,26 +236,22 @@ def tile_picked_mixup_none_lo_kernel(tc, xT, w1, w2, lam, mu, offs, pos1, out_0,
             nc.vector.quantize_mx(y_codes[c][:].bitcast(FP8X4), y_scales[:, j0 : j0 + n], y_bf[c][:].rearrange("p n t -> p (n t)"))
             nc.sync.dma_start(y_words[:, j0 : j0 + n], y_codes[c][:].bitcast(I32))
 
-        mix(0)
-        nc.vector.quantize_mx(w2_codes[:].bitcast(FP8X4), w2_scales[:], w2_bf[:].rearrange("p t m j -> p (t m j)"))
+        mix(0, 0)
+        mix(0, 1)
+        mix(1, 2)
         quantise_z(0)
         second_layer(0)
         round_y(0, nc.scalar.copy)
-        late = keep.tile([P, 2, PACK, CHUNKS[1][1]], F32, name="partner_late", tag="late", align_bytes=64)
-        partner.extend([late[:, 0, :, :], late[:, 1, :, :]])
-        for t in range(PACK):
-            gather_h(1, t)
-        mix(1)
-        gather_h(2, 0)
+        partner.append(keep.tile([P, PACK, GATHERS[1][1]], F32, name="partner1", tag="partner"))
         quantise_z(1)
         second_layer(1)
-        round_y(1, nc.scalar.copy)
-        for t in range(1, PACK):
-            gather_h(2, t)
-        mix(2)
+        for t in range(PACK):
+            gather_h(1, t)
+        mix(2, 3)
         quantise_y(0)
         quantise_z(2)
         second_layer(2)
+        round_y(1, nc.vector.tensor_copy)
         quantise_y(1)
         round_y(2, nc.vector.tensor_copy)
         quantise_y(2)

@@ -24,7 +24,7 @@ HALF = S // 2
 CHUNKS = ((0, 256), (256, 128), (384, 128))
 GATHERS = ((0, 384), (384, 128))
 W1_SPLIT = 104
-W2_SPLIT = 44
+W2_SPLIT = 56
 
 
 def tile_picked_mixup_none_lo_kernel(tc, xT, w1, w2, lam, mu, offs, pos1, out_0, out_1, out_2):
@@ -54,10 +54,10 @@ def tile_picked_mixup_none_lo_kernel(tc, xT, w1, w2, lam, mu, offs, pos1, out_0,
         for u in range(2):
             nc.sync.dma_start(w1_half[u][:], w1_rows[:, :, u * HALF : (u + 1) * HALF])
         nc.sync.dma_start(w2_half[0][:], w2_rows[:, :, 0:HALF])
-        nc.sync.dma_start(lam_rows[:], lam.rearrange("r (b m) -> (r b) m", m=P)[0:P, :])
-        nc.sync.dma_start(mu_part[0][:], mu[:, 0 : GATHERS[0][1]])
-        nc.sync.dma_start(pos_sb[:], pos1)
         nc.sync.dma_start(w2_half[1][:], w2_rows[:, :, HALF:S])
+        nc.sync.dma_start(pos_sb[:], pos1)
+        nc.sync.dma_start(mu_part[0][:], mu[:, 0 : GATHERS[0][1]])
+        nc.sync.dma_start(lam_rows[:], lam.rearrange("r (b m) -> (r b) m", m=P)[0:P, :])
         nc.sync.dma_start(mu_part[1][:], mu[:, GATHERS[1][0] : S])
 
         def deal(copy, dst, src, m0, m1):
@@ -124,16 +124,16 @@ def tile_picked_mixup_none_lo_kernel(tc, xT, w1, w2, lam, mu, offs, pos1, out_0,
             else:
                 h_banks.append((t, slice(0, S), first_layer(t, slice(0, S), f"bank{t + 1}")))
 
-        lam_ps = psum.tile([P, P], F32, name="lam_ps", tag="bank7")
-        lam_col = keep.tile([P, PACK], F32, name="lam_col")
-        nc.tensor.transpose(lam_ps[:], lam_rows[:], identity[:])
-        nc.scalar.copy(lam_col[:], lam_ps[:, 0:PACK])
-
         deal(nc.vector.tensor_copy, w2_bf, w2_half, W2_SPLIT, P // 2)
         deal(nc.vector.tensor_copy, w2_bf, w2_half, P // 2, P)
 
         for t, cols_j, h_ps in h_banks:
             nc.scalar.copy(h_sb[t][:, cols_j], h_ps[:])
+
+        lam_ps = psum.tile([P, P], F32, name="lam_ps", tag="bank7")
+        lam_col = keep.tile([P, PACK], F32, name="lam_col")
+        nc.tensor.transpose(lam_ps[:], lam_rows[:], identity[:])
+        nc.scalar.copy(lam_col[:], lam_ps[:, 0:PACK])
 
         partner = [keep.tile([P, PACK, GATHERS[0][1]], F32, name="partner0", tag="partner")]
 
@@ -146,9 +146,8 @@ def tile_picked_mixup_none_lo_kernel(tc, xT, w1, w2, lam, mu, offs, pos1, out_0,
                 MULT,
             )
 
-        gather_h(0, 0)
         nc.vector.quantize_mx(w2_codes[:].bitcast(FP8X4), w2_scales[:], w2_bf[:].rearrange("p t m j -> p (t m j)"))
-        for t in range(1, PACK):
+        for t in range(PACK):
             gather_h(0, t)
 
         turned_tags = ["bank5", "bank6", "bank0", "bank1"]
@@ -223,7 +222,10 @@ def tile_picked_mixup_none_lo_kernel(tc, xT, w1, w2, lam, mu, offs, pos1, out_0,
                         stop=True,
                     )
                 nc.scalar.copy(y_sb[c][:, 2 * u : 2 * u + 2, :], bank[:])
-            nc.sync.dma_start(y_rows[:, :, j0 : j0 + n], y_sb[c][:])
+                if c == 0:
+                    nc.sync.dma_start(y_rows[:, 2 * u : 2 * u + 2, j0 : j0 + n], y_sb[c][:, 2 * u : 2 * u + 2, :])
+            if c > 0:
+                nc.sync.dma_start(y_rows[:, :, j0 : j0 + n], y_sb[c][:])
 
         def round_y(c, copy):
             copy(
@@ -241,18 +243,18 @@ def tile_picked_mixup_none_lo_kernel(tc, xT, w1, w2, lam, mu, offs, pos1, out_0,
         mix(1, 2)
         quantise_z(0)
         second_layer(0)
-        round_y(0, nc.scalar.copy)
         partner.append(keep.tile([P, PACK, GATHERS[1][1]], F32, name="partner1", tag="partner"))
         quantise_z(1)
         second_layer(1)
+        round_y(0, nc.scalar.copy)
         for t in range(PACK):
             gather_h(1, t)
         mix(2, 3)
-        quantise_y(0)
+        round_y(1, nc.vector.tensor_copy)
         quantise_z(2)
         second_layer(2)
-        round_y(1, nc.vector.tensor_copy)
         quantise_y(1)
+        quantise_y(0)
         round_y(2, nc.vector.tensor_copy)
         quantise_y(2)
         for q in range(4):

@@ -43,7 +43,7 @@ def tile_picked_mixup_none_lo_kernel(tc, xT, w1, w2, lam, mu, offs, pos1, out_0,
         w1_half = [keep.tile([P, PACK, HALF], F32, name=f"w1_half{u}") for u in range(2)]
         w2_half = [keep.tile([P, PACK, HALF], F32, name=f"w2_half{u}") for u in range(2)]
         lam_rows = keep.tile([P, P], F32, name="lam_rows")
-        mu_part = [keep.tile([P, n], F32, name=f"mu_part{g}") for g, (j0, n) in enumerate(GATHERS)]
+        mu_part = [keep.tile([P, n], F32, name=f"mu_part{g}", tag=f"mu_part{g}", align_bytes=64) for g, (j0, n) in enumerate(GATHERS)]
         identity = keep.tile([P, P], F32, name="identity")
         make_identity(nc, identity[:])
 
@@ -76,7 +76,6 @@ def tile_picked_mixup_none_lo_kernel(tc, xT, w1, w2, lam, mu, offs, pos1, out_0,
         w1_codes = keep.tile([P, H], U32, name="w1_codes", align_bytes=64)
         w1_scales = keep.tile([P, H], U8, name="w1_scales", align_bytes=64)
         w2_bf = keep.tile([P, PACK, P, PACK], BF16, name="w2_bf", align_bytes=64)
-        w2_codes = keep.tile([P, H], U32, name="w2_codes", align_bytes=64)
         w2_scales = keep.tile([P, H], U8, name="w2_scales", align_bytes=64)
         halves = [slice(0, HALF), slice(HALF, S)]
 
@@ -146,9 +145,10 @@ def tile_picked_mixup_none_lo_kernel(tc, xT, w1, w2, lam, mu, offs, pos1, out_0,
                 MULT,
             )
 
-        nc.vector.quantize_mx(w2_codes[:].bitcast(FP8X4), w2_scales[:], w2_bf[:].rearrange("p t m j -> p (t m j)"))
         for t in range(PACK):
             gather_h(0, t)
+        w2_codes = keep.tile([P, H], U32, name="w2_codes", tag="mu_part0", align_bytes=64)
+        nc.vector.quantize_mx(w2_codes[:].bitcast(FP8X4), w2_scales[:], w2_bf[:].rearrange("p t m j -> p (t m j)"))
 
         turned_tags = ["bank5", "bank6", "bank0", "bank1"]
         own_tags = ["bank2", "bank3", "bank4", "bank7"]

@@ -19,7 +19,7 @@ COPY = mybir.ActivationFunctionType.Copy
 
 P = 128
 PACK = 4
-RUN = 2
+RUN = 4
 HALF = S // 2
 CHUNKS = ((0, 256), (256, 128), (384, 128))
 GATHERS = ((0, 384), (384, 128))
@@ -136,17 +136,17 @@ def tile_picked_mixup_none_lo_kernel(tc, xT, w1, w2, lam, mu, offs, pos1, out_0,
 
         partner = [keep.tile([P, PACK, GATHERS[0][1]], F32, name="partner0", tag="partner")]
 
-        def gather_h(c, t):
-            j0, n = GATHERS[c]
+        def gather_h(c, t, a, b):
+            j0 = GATHERS[c][0]
             nc.vector.tensor_tensor(
-                partner[c][:, t, :],
-                h_sb[t][:].indirect(pos_sb[:, j0 // 16 : (j0 + n) // 16]),
-                mu_part[c][:],
+                partner[c][:, t, a:b],
+                h_sb[t][:].indirect(pos_sb[:, (j0 + a) // 16 : (j0 + b) // 16]),
+                mu_part[c][:, a:b],
                 MULT,
             )
 
         for t in range(PACK):
-            gather_h(0, t)
+            gather_h(0, t, 0, GATHERS[0][1])
         w2_codes = keep.tile([P, H], U32, name="w2_codes", tag="mu_part0", align_bytes=64)
         nc.vector.quantize_mx(w2_codes[:].bitcast(FP8X4), w2_scales[:], w2_bf[:].rearrange("p t m j -> p (t m j)"))
 
@@ -190,14 +190,14 @@ def tile_picked_mixup_none_lo_kernel(tc, xT, w1, w2, lam, mu, offs, pos1, out_0,
             y_bf.append(keep.tile([P, n, PACK], BF16, name=f"y_bf{c}", align_bytes=64))
             y_codes.append(keep.tile([P, n], U32, name=f"y_codes{c}", align_bytes=64))
 
-        def mix(c, b):
+        def mix(c, b, a0, a1):
             j0 = P * b - CHUNKS[c][0]
             g = b // 3
             g0 = P * b - GATHERS[g][0]
             nc.vector.tensor_tensor(
-                z_bf[c][:, j0 : j0 + P, :].rearrange("p (g i) t -> p g t i", i=RUN),
-                own_ps[b][:].rearrange("p t (g i) -> p g t i", i=RUN),
-                partner[g][:, :, g0 : g0 + P].rearrange("p t (g i) -> p g t i", i=RUN),
+                z_bf[c][:, j0 + a0 : j0 + a1, :].rearrange("p (g i) t -> p g t i", i=RUN),
+                own_ps[b][:, :, a0:a1].rearrange("p t (g i) -> p g t i", i=RUN),
+                partner[g][:, :, g0 + a0 : g0 + a1].rearrange("p t (g i) -> p g t i", i=RUN),
                 ADD,
             )
 
@@ -238,24 +238,28 @@ def tile_picked_mixup_none_lo_kernel(tc, xT, w1, w2, lam, mu, offs, pos1, out_0,
             nc.vector.quantize_mx(y_codes[c][:].bitcast(FP8X4), y_scales[:, j0 : j0 + n], y_bf[c][:].rearrange("p n t -> p (n t)"))
             nc.sync.dma_start(y_words[:, j0 : j0 + n], y_codes[c][:].bitcast(I32))
 
-        mix(0, 0)
-        mix(0, 1)
-        mix(1, 2)
+        mix(0, 0, 0, P)
+        mix(0, 1, 0, P)
+        mix(1, 2, 0, P)
         quantise_z(0)
         second_layer(0)
         partner.append(keep.tile([P, PACK, GATHERS[1][1]], F32, name="partner1", tag="partner"))
         quantise_z(1)
         second_layer(1)
         round_y(0, nc.scalar.copy)
-        for t in range(PACK):
-            gather_h(1, t)
-        mix(2, 3)
+        for t in range(PACK - 1):
+            gather_h(1, t, 0, P)
+        for a in range(0, P, P // 2):
+            gather_h(1, PACK - 1, a, a + P // 2)
+        for a in range(0, P, P // 2):
+            mix(2, 3, a, a + P // 2)
         round_y(1, nc.vector.tensor_copy)
         quantise_z(2)
         second_layer(2)
         quantise_y(1)
         quantise_y(0)
-        round_y(2, nc.vector.tensor_copy)
+        for u in range(2):
+            nc.vector.tensor_copy(y_bf[2][:, :, 2 * u : 2 * u + 2], y_sb[2][:, 2 * u : 2 * u + 2, :].rearrange("p e n -> p n e"))
         quantise_y(2)
         for q in range(4):
             queue = nc.sync if q % 2 == 0 else nc.scalar

@@ -46,6 +46,8 @@ def tile_picked_mixup_none_lo_kernel(tc, xT, w1, w2, lam, mu, offs, pos1, out_0,
         mu_part = [keep.tile([P, n], F32, name=f"mu_part{g}", tag=f"mu_part{g}", align_bytes=64) for g, (j0, n) in enumerate(GATHERS)]
         identity = keep.tile([P, P], F32, name="identity")
         make_identity(nc, identity[:])
+        late_identity = keep.tile([P, P], F32, name="late_identity", tag="w2_codes", align_bytes=64)
+        make_identity(nc, late_identity[:])
 
         nc.sync.dma_start(x_plane[0][:], x_rows[:, 0, :])
         nc.sync.dma_start(offs_sb[:], offs)
@@ -147,8 +149,6 @@ def tile_picked_mixup_none_lo_kernel(tc, xT, w1, w2, lam, mu, offs, pos1, out_0,
 
         for t in range(PACK):
             gather_h(0, t, 0, GATHERS[0][1])
-        w2_codes = keep.tile([P, H], U32, name="w2_codes", tag="mu_part0", align_bytes=64)
-        nc.vector.quantize_mx(w2_codes[:].bitcast(FP8X4), w2_scales[:], w2_bf[:].rearrange("p t m j -> p (t m j)"))
 
         turned_tags = ["bank5", "bank6", "bank0", "bank1"]
         own_tags = ["bank2", "bank3", "bank4", "bank7"]
@@ -157,7 +157,8 @@ def tile_picked_mixup_none_lo_kernel(tc, xT, w1, w2, lam, mu, offs, pos1, out_0,
         def turn(b):
             turned = psum.tile([P, PACK, P], F32, name=f"turned{b}", tag=turned_tags[b])
             for t in range(PACK):
-                nc.tensor.transpose(turned[:, t, :], h_sb[t][:, P * b : P * (b + 1)], identity[:])
+                ident = late_identity if (b, t) == (0, PACK - 1) else identity
+                nc.tensor.transpose(turned[:, t, :], h_sb[t][:, P * b : P * (b + 1)], ident[:])
             return turned
 
         def scale_and_turn_back(b, turned):
@@ -169,6 +170,8 @@ def tile_picked_mixup_none_lo_kernel(tc, xT, w1, w2, lam, mu, offs, pos1, out_0,
             own_ps.append(own)
 
         turned = [turn(0), turn(1)]
+        w2_codes = keep.tile([P, H], U32, name="w2_codes", tag="w2_codes", align_bytes=64)
+        nc.vector.quantize_mx(w2_codes[:].bitcast(FP8X4), w2_scales[:], w2_bf[:].rearrange("p t m j -> p (t m j)"))
         scale_and_turn_back(0, turned[0])
         turned.append(turn(2))
         scale_and_turn_back(1, turned[1])

@@ -22,9 +22,10 @@ PACK = 4
 RUN = 4
 HALF = S // 2
 CHUNKS = ((0, 256), (256, 128), (384, 128))
-GATHERS = ((0, 384), (384, 128))
+GATHERS = ((0, 416), (416, 96))
 W1_SPLIT = 104
 W2_SPLIT = 56
+Y_SPLIT = 144
 
 
 def tile_picked_mixup_none_lo_kernel(tc, xT, w1, w2, lam, mu, offs, pos1, out_0, out_1, out_2):
@@ -184,18 +185,19 @@ def tile_picked_mixup_none_lo_kernel(tc, xT, w1, w2, lam, mu, offs, pos1, out_0,
         y_scale_rows = out_2.rearrange("z q c -> q (z c)").bitcast(I32)
         y_scales = keep.tile([P, S], U8, name="y_scales", align_bytes=64)
 
-        z_bf, z_codes, z_scales, y_sb, y_bf, y_codes = [], [], [], [], [], []
+        z_bf, z_codes, z_scales, y_sb, y_bf, y_codes = [], [], [], [], {}, []
         for c, (j0, n) in enumerate(CHUNKS):
-            z_bf.append(keep.tile([P, n, PACK], BF16, name=f"z_bf{c}", align_bytes=64))
+            z_bf.append(keep.tile([P, n, PACK], BF16, name=f"z_bf{c}", tag=f"z_bf{c}", align_bytes=64))
             z_codes.append(keep.tile([P, n], U32, name=f"z_codes{c}", align_bytes=64))
             z_scales.append(keep.tile([P, n], U8, name=f"z_scales{c}", align_bytes=64))
             y_sb.append(keep.tile([P, PACK, n], F32, name=f"y_sb{c}"))
-            y_bf.append(keep.tile([P, n, PACK], BF16, name=f"y_bf{c}", align_bytes=64))
+            if c != 1:
+                y_bf[c] = keep.tile([P, n, PACK], BF16, name=f"y_bf{c}", align_bytes=64)
             y_codes.append(keep.tile([P, n], U32, name=f"y_codes{c}", align_bytes=64))
 
         def mix(c, b, a0, a1):
             j0 = P * b - CHUNKS[c][0]
-            g = b // 3
+            g = 0 if P * b + a0 < GATHERS[1][0] else 1
             g0 = P * b - GATHERS[g][0]
             nc.vector.tensor_tensor(
                 z_bf[c][:, j0 + a0 : j0 + a1, :].rearrange("p (g i) t -> p g t i", i=RUN),
@@ -230,10 +232,10 @@ def tile_picked_mixup_none_lo_kernel(tc, xT, w1, w2, lam, mu, offs, pos1, out_0,
             if c > 0:
                 nc.sync.dma_start(y_rows[:, :, j0 : j0 + n], y_sb[c][:])
 
-        def round_y(c, copy):
+        def round_y(c, copy, a0, a1):
             copy(
-                y_bf[c][:].rearrange("p (g i) t -> p g t i", i=RUN),
-                y_sb[c][:].rearrange("p t (g i) -> p g t i", i=RUN),
+                y_bf[c][:, a0:a1, :].rearrange("p (g i) t -> p g t i", i=RUN),
+                y_sb[c][:, :, a0:a1].rearrange("p t (g i) -> p g t i", i=RUN),
             )
 
         def quantise_y(c):
@@ -246,21 +248,21 @@ def tile_picked_mixup_none_lo_kernel(tc, xT, w1, w2, lam, mu, offs, pos1, out_0,
         mix(1, 2, 0, P)
         quantise_z(0)
         second_layer(0)
-        partner.append(keep.tile([P, PACK, GATHERS[1][1]], F32, name="partner1", tag="partner"))
+        partner.append(keep.tile([P, PACK, GATHERS[1][1]], F32, name="partner1", tag="z_bf0", align_bytes=64))
         quantise_z(1)
         second_layer(1)
-        round_y(0, nc.scalar.copy)
-        for t in range(PACK - 1):
-            gather_h(1, t, 0, P)
-        for a in range(0, P, P // 2):
-            gather_h(1, PACK - 1, a, a + P // 2)
-        for a in range(0, P, P // 2):
-            mix(2, 3, a, a + P // 2)
-        round_y(1, nc.vector.tensor_copy)
+        round_y(0, nc.scalar.copy, 0, Y_SPLIT)
+        for t in range(PACK):
+            gather_h(1, t, 0, GATHERS[1][1])
+        mix(2, 3, 0, P - GATHERS[1][1])
+        mix(2, 3, P - GATHERS[1][1], P)
+        round_y(0, nc.vector.tensor_copy, Y_SPLIT, CHUNKS[0][1])
         quantise_z(2)
         second_layer(2)
-        quantise_y(1)
+        y_bf[1] = keep.tile([P, P, PACK], BF16, name="y_bf1", tag="z_bf2", align_bytes=64)
+        round_y(1, nc.vector.tensor_copy, 0, P)
         quantise_y(0)
+        quantise_y(1)
         for u in range(2):
             nc.vector.tensor_copy(y_bf[2][:, :, 2 * u : 2 * u + 2], y_sb[2][:, 2 * u : 2 * u + 2, :].rearrange("p e n -> p n e"))
         quantise_y(2)

@@ -25,7 +25,8 @@ CHUNKS = ((0, 256), (256, 128), (384, 128))
 GATHERS = ((0, 416), (416, 96))
 W1_SPLIT = 104
 W2_SPLIT = 56
-Y_SPLIT = 144
+Y_SPLIT = 128
+Y_CHUNKS = ((0, 128), (128, 256), (384, 128))
 
 
 def tile_picked_mixup_none_lo_kernel(tc, xT, w1, w2, lam, mu, offs, pos1, out_0, out_1, out_2):
@@ -192,8 +193,8 @@ def tile_picked_mixup_none_lo_kernel(tc, xT, w1, w2, lam, mu, offs, pos1, out_0,
             z_scales.append(keep.tile([P, n], U8, name=f"z_scales{c}", align_bytes=64))
             y_sb.append(keep.tile([P, PACK, n], F32, name=f"y_sb{c}"))
             if c != 1:
-                y_bf[c] = keep.tile([P, n, PACK], BF16, name=f"y_bf{c}", align_bytes=64)
-            y_codes.append(keep.tile([P, n], U32, name=f"y_codes{c}", align_bytes=64))
+                y_bf[c] = keep.tile([P, P, PACK], BF16, name=f"y_bf{c}", align_bytes=64)
+            y_codes.append(keep.tile([P, Y_CHUNKS[c][1]], U32, name=f"y_codes{c}", align_bytes=64))
 
         def mix(c, b, a0, a1):
             j0 = P * b - CHUNKS[c][0]
@@ -239,7 +240,7 @@ def tile_picked_mixup_none_lo_kernel(tc, xT, w1, w2, lam, mu, offs, pos1, out_0,
             )
 
         def quantise_y(c):
-            j0, n = CHUNKS[c]
+            j0, n = Y_CHUNKS[c]
             nc.vector.quantize_mx(y_codes[c][:].bitcast(FP8X4), y_scales[:, j0 : j0 + n], y_bf[c][:].rearrange("p n t -> p (n t)"))
             nc.sync.dma_start(y_words[:, j0 : j0 + n], y_codes[c][:].bitcast(I32))
 
@@ -255,17 +256,25 @@ def tile_picked_mixup_none_lo_kernel(tc, xT, w1, w2, lam, mu, offs, pos1, out_0,
         for t in range(PACK):
             gather_h(1, t, 0, GATHERS[1][1])
         mix(2, 3, 0, P - GATHERS[1][1])
-        mix(2, 3, P - GATHERS[1][1], P)
-        round_y(0, nc.vector.tensor_copy, Y_SPLIT, CHUNKS[0][1])
-        quantise_z(2)
+        mix(2, 3, P - GATHERS[1][1], P // 2)
+        mix(2, 3, P // 2, P)
+        for a in range(0, P, P // 2):
+            nc.vector.quantize_mx(
+                z_codes[2][:, a : a + P // 2].bitcast(FP8X4),
+                z_scales[2][:, a : a + P // 2],
+                z_bf[2][:, a : a + P // 2, :].rearrange("p n t -> p (n t)"),
+            )
         second_layer(2)
-        y_bf[1] = keep.tile([P, P, PACK], BF16, name="y_bf1", tag="z_bf2", align_bytes=64)
-        round_y(1, nc.vector.tensor_copy, 0, P)
+        y_bf[1] = keep.tile([P, CHUNKS[0][1] - Y_SPLIT + P, PACK], BF16, name="y_bf1", tag="z_bf2", align_bytes=64)
+        for c, a0, b0 in ((0, Y_SPLIT, 0), (1, 0, P)):
+            nc.vector.tensor_copy(
+                y_bf[1][:, b0 : b0 + P, :].rearrange("p (g i) t -> p g t i", i=RUN),
+                y_sb[c][:, :, a0 : a0 + P].rearrange("p t (g i) -> p g t i", i=RUN),
+            )
         quantise_y(0)
         quantise_y(1)
         for u in range(2):
             nc.vector.tensor_copy(y_bf[2][:, :, 2 * u : 2 * u + 2], y_sb[2][:, 2 * u : 2 * u + 2, :].rearrange("p e n -> p n e"))
         quantise_y(2)
         for q in range(4):
-            queue = nc.sync if q % 2 == 0 else nc.scalar
-            queue.dma_start(y_scale_rows[4 * q : 4 * q + 4, :], y_scales[32 * q : 32 * q + 4, :].bitcast(I32))
+            nc.sync.dma_start(y_scale_rows[4 * q : 4 * q + 4, :], y_scales[32 * q : 32 * q + 4, :].bitcast(I32))

@@ -21,12 +21,7 @@ P = 128
 PACK = 4
 RUN = 4
 HALF = S // 2
-CHUNKS = ((0, 256), (256, 128), (384, 128))
-GATHERS = ((0, 416), (416, 96))
-W1_SPLIT = 104
-W2_SPLIT = 56
-Y_SPLIT = 128
-Y_CHUNKS = ((0, 128), (128, 256), (384, 128))
+M_HALF = P // 2
 
 
 def tile_picked_mixup_none_lo_kernel(tc, xT, w1, w2, lam, mu, offs, pos1, out_0, out_1, out_2):
@@ -35,246 +30,248 @@ def tile_picked_mixup_none_lo_kernel(tc, xT, w1, w2, lam, mu, offs, pos1, out_0,
         keep = ctx.enter_context(tc.tile_pool(name="keep", bufs=1))
         psum = ctx.enter_context(tc.psum_pool(name="psum", bufs=1))
 
+        def sb(name, shape, dtype, tag=None):
+            return keep.tile(shape, dtype, name=name, tag=tag or name, align_bytes=64)
+
+        def bank(name, shape, number):
+            return psum.tile(shape, F32, name=name, tag=f"bank{number}")
+
         offs_sb = keep.tile([P, S // 16], U16, name="offs_sb")
         pos_sb = keep.tile([P, S // 16], U16, name="pos_sb")
+        zero = sb("zero", [P, 1], F32)
+        nc.gpsimd.memset(zero[:], 0.0)
+        share_rows = sb("share_rows", [P, P], F32)
+        nc.scalar.copy(share_rows[:], zero[:].to_broadcast([P, P]))
+        identity = sb("identity", [P, P], F32)
+        make_identity(nc, identity[:])
+        late_identity = sb("late_identity", [P, P], F32)
+        make_identity(nc, late_identity[:])
+
         x_rows = xT.rearrange("(p t) n -> p t n", t=PACK)
         w1_rows = w1.rearrange("(p j) c -> p j c", j=PACK)
         w2_rows = w2.rearrange("(p j) c -> p j c", j=PACK)
+        halves = [slice(0, HALF), slice(HALF, S)]
 
-        x_plane = [keep.tile([P, T], F32, name=f"x_plane{t}") for t in range(PACK)]
-        w1_half = [keep.tile([P, PACK, HALF], F32, name=f"w1_half{u}") for u in range(2)]
-        w2_half = [keep.tile([P, PACK, HALF], F32, name=f"w2_half{u}") for u in range(2)]
-        lam_rows = keep.tile([P, P], F32, name="lam_rows")
-        mu_part = [keep.tile([P, n], F32, name=f"mu_part{g}", tag=f"mu_part{g}", align_bytes=64) for g, (j0, n) in enumerate(GATHERS)]
-        identity = keep.tile([P, P], F32, name="identity")
-        make_identity(nc, identity[:])
-        late_identity = keep.tile([P, P], F32, name="late_identity", tag="w2_codes", align_bytes=64)
-        make_identity(nc, late_identity[:])
+        x_plane = [sb(f"x_plane{t}", [P, T], F32) for t in range(PACK)]
+        w1_raw = [sb(f"w1_raw{u}", [P, PACK, HALF], F32) for u in range(2)]
+        mu_rows = sb("mu_rows", [P, 3 * P], F32)
 
         nc.sync.dma_start(x_plane[0][:], x_rows[:, 0, :])
         nc.sync.dma_start(offs_sb[:], offs)
         for t in range(1, PACK):
             nc.sync.dma_start(x_plane[t][:], x_rows[:, t, :])
         for u in range(2):
-            nc.sync.dma_start(w1_half[u][:], w1_rows[:, :, u * HALF : (u + 1) * HALF])
-        nc.sync.dma_start(w2_half[0][:], w2_rows[:, :, 0:HALF])
-        nc.sync.dma_start(w2_half[1][:], w2_rows[:, :, HALF:S])
+            nc.sync.dma_start(w1_raw[u][:], w1_rows[:, :, halves[u]])
+        w2_raw = [sb("w2_raw0", [P, PACK, HALF], F32)]
+        nc.sync.dma_start(w2_raw[0][:], w2_rows[:, :, halves[0]])
         nc.sync.dma_start(pos_sb[:], pos1)
-        nc.sync.dma_start(mu_part[0][:], mu[:, 0 : GATHERS[0][1]])
-        nc.sync.dma_start(lam_rows[:], lam.rearrange("r (b m) -> (r b) m", m=P)[0:P, :])
-        nc.sync.dma_start(mu_part[1][:], mu[:, GATHERS[1][0] : S])
+        nc.sync.dma_start(mu_rows[:], mu[:, P:S])
+        for g, share in enumerate((lam, mu)):
+            nc.sync.dma_start(share_rows[PACK * g : PACK * (g + 1), :], share[0:1, :].rearrange("r (b m) -> (r b) m", m=P))
 
-        def deal(copy, dst, src, m0, m1):
-            u = m0 // (P // 2)
-            base = u * (P // 2)
-            copy(
-                dst[:, :, m0:m1, :].rearrange("p t m j -> p m j t"),
-                src[u][:, :, PACK * (m0 - base) : PACK * (m1 - base)].rearrange("p j (m t) -> p m j t", t=PACK),
-            )
+        def quantise(codes, scales, values):
+            nc.vector.quantize_mx(codes.bitcast(FP8X4), scales, values)
 
-        x_pair = [keep.tile([P, 2, S], F32, name=f"x_pair{u}") for u in range(2)]
-        x_bf = keep.tile([P, S, PACK], BF16, name="x_bf", align_bytes=64)
-        x_codes = keep.tile([P, S], U32, name="x_codes", align_bytes=64)
-        x_scales = keep.tile([P, S], U8, name="x_scales", align_bytes=64)
-        w1_bf = keep.tile([P, PACK, P, PACK], BF16, name="w1_bf", align_bytes=64)
-        w1_codes = keep.tile([P, H], U32, name="w1_codes", align_bytes=64)
-        w1_scales = keep.tile([P, H], U8, name="w1_scales", align_bytes=64)
-        w2_bf = keep.tile([P, PACK, P, PACK], BF16, name="w2_bf", align_bytes=64)
-        w2_scales = keep.tile([P, H], U8, name="w2_scales", align_bytes=64)
-        halves = [slice(0, HALF), slice(HALF, S)]
-
-        def gather_x(t, j0, j1):
-            nc.vector.tensor_copy(x_pair[t // 2][:, t % 2, j0:j1], x_plane[t][:].indirect(offs_sb[:, j0 // 16 : j1 // 16]))
-
-        gather_x(0, 0, S)
-        gather_x(1, 0, S)
-        nc.scalar.copy(x_bf[:, :, 0:2], x_pair[0][:].rearrange("p e n -> p n e"))
-        gather_x(2, 0, S)
-        gather_x(3, 0, HALF)
-        gather_x(3, HALF, S)
-        for half in halves:
-            nc.vector.tensor_copy(x_bf[:, half, 2:4], x_pair[1][:, :, half].rearrange("p e n -> p n e"))
-        deal(nc.scalar.copy, w1_bf, w1_half, 0, P // 2)
-        for half in halves:
-            nc.vector.quantize_mx(x_codes[:, half].bitcast(FP8X4), x_scales[:, half], x_bf[:, half, :].rearrange("p n t -> p (n t)"))
-        deal(nc.scalar.copy, w1_bf, w1_half, P // 2, W1_SPLIT)
-        deal(nc.vector.tensor_copy, w1_bf, w1_half, W1_SPLIT, P)
-        deal(nc.scalar.copy, w2_bf, w2_half, 0, W2_SPLIT)
-
-        h_sb = [keep.tile([P, S], F32, name=f"h_sb{t}") for t in range(PACK)]
-
-        def first_layer(t, cols_j, tag):
+        def product(out, w_codes, w_scales, t, codes, scales):
             cols = slice(P * t, P * (t + 1))
-            h_ps = psum.tile([P, cols_j.stop - cols_j.start], F32, name=f"h_ps_{tag}", tag=tag)
             nc.tensor.matmul_mx(
-                out=h_ps[:],
-                lhsT=w1_codes[:, cols].bitcast(FP8X4),
-                lhsT_scale=w1_scales[:, cols],
-                rhs=x_codes[:, cols_j].bitcast(FP8X4),
-                rhs_scale=x_scales[:, cols_j],
+                out=out,
+                lhsT=w_codes[:, cols].bitcast(FP8X4),
+                lhsT_scale=w_scales[:, cols],
+                rhs=codes.bitcast(FP8X4),
+                rhs_scale=scales,
                 start=True,
                 stop=True,
             )
-            return h_ps
 
-        h_banks = []
-        for t in range(PACK):
-            cols = slice(P * t, P * (t + 1))
-            nc.vector.quantize_mx(w1_codes[:, cols].bitcast(FP8X4), w1_scales[:, cols], w1_bf[:, t, :, :].rearrange("p m j -> p (m j)"))
-            if t == 0:
-                for u, half in enumerate(halves):
-                    h_banks.append((t, half, first_layer(t, half, f"bank{u}")))
-            else:
-                h_banks.append((t, slice(0, S), first_layer(t, slice(0, S), f"bank{t + 1}")))
+        def deal(copy, dst, src):
+            copy(dst.rearrange("p t m j -> p m j t"), src.rearrange("p j (m t) -> p m j t", t=PACK))
 
-        deal(nc.vector.tensor_copy, w2_bf, w2_half, W2_SPLIT, P // 2)
-        deal(nc.vector.tensor_copy, w2_bf, w2_half, P // 2, P)
+        def walk(ap):
+            return ap.rearrange("p t (g i) -> p g t i", i=RUN)
 
-        for t, cols_j, h_ps in h_banks:
-            nc.scalar.copy(h_sb[t][:, cols_j], h_ps[:])
+        def walk_packed(ap):
+            return ap.rearrange("p (g i) t -> p g t i", i=RUN)
 
-        lam_ps = psum.tile([P, P], F32, name="lam_ps", tag="bank7")
-        lam_col = keep.tile([P, PACK], F32, name="lam_col")
-        nc.tensor.transpose(lam_ps[:], lam_rows[:], identity[:])
-        nc.scalar.copy(lam_col[:], lam_ps[:, 0:PACK])
+        x_bf = sb("x_bf", [P, S, PACK], BF16)
+        x_codes = sb("x_codes", [P, S], U32)
+        x_scales = sb("x_scales", [P, S], U8)
 
-        partner = [keep.tile([P, PACK, GATHERS[0][1]], F32, name="partner0", tag="partner")]
+        def gather_plane(pair, t):
+            nc.vector.tensor_copy(pair[0][:, t % 2, :], x_plane[t][:].indirect(offs_sb[:, 0 : HALF // 16]))
+            nc.scalar.activation(pair[1][:, t % 2, :], x_plane[t][:].indirect(offs_sb[:, HALF // 16 : S // 16]), COPY)
 
-        def gather_h(c, t, a, b):
-            j0 = GATHERS[c][0]
-            nc.vector.tensor_tensor(
-                partner[c][:, t, a:b],
-                h_sb[t][:].indirect(pos_sb[:, (j0 + a) // 16 : (j0 + b) // 16]),
-                mu_part[c][:, a:b],
-                MULT,
+        pair0 = [sb(f"pair0{u}", [P, 2, HALF], F32, tag=f"x_pair0{u}") for u in range(2)]
+        gather_plane(pair0, 0)
+        gather_plane(pair0, 1)
+        for u, half in enumerate(halves):
+            nc.vector.tensor_copy(walk_packed(x_bf[:, half, 0:2]), walk(pair0[u][:]))
+        pair1 = [sb("pair10", [P, 2, HALF], F32, tag="x_pair00"), sb("pair11", [P, 2, HALF], F32, tag="x_pair11")]
+        gather_plane(pair1, 2)
+        gather_plane(pair1, 3)
+        for u, half in enumerate(halves):
+            nc.vector.tensor_copy(walk_packed(x_bf[:, half, 2:4]), walk(pair1[u][:]))
+        w1_bf = [sb("w1_bf0", [P, PACK, M_HALF, PACK], BF16, tag="x_plane3")]
+        deal(nc.scalar.copy, w1_bf[0][:], w1_raw[0][:])
+        for half in halves:
+            quantise(x_codes[:, half], x_scales[:, half], x_bf[:, half, :].rearrange("p n t -> p (n t)"))
+        w1_bf.append(sb("w1_bf1", [P, PACK, M_HALF, PACK], BF16, tag="x_pair11"))
+
+        def deal_w1_pair(u):
+            nc.vector.tensor_copy(
+                w1_bf[1][:, 2 * u : 2 * u + 2, :, :].rearrange("p t m j -> p m j t"),
+                w1_raw[1][:].rearrange("p j (m t) -> p m j t", t=PACK)[:, :, :, 2 * u : 2 * u + 2],
             )
 
-        for t in range(PACK):
-            gather_h(0, t, 0, GATHERS[0][1])
 
-        turned_tags = ["bank5", "bank6", "bank0", "bank1"]
-        own_tags = ["bank2", "bank3", "bank4", "bank7"]
-        own_ps = []
+        w1_codes = sb("w1_codes", [P, H], U32)
+        w1_scales = sb("w1_scales", [P, H], U8)
 
-        def turn(b):
-            turned = psum.tile([P, PACK, P], F32, name=f"turned{b}", tag=turned_tags[b])
+        def quantise_w1(t, u):
+            cols = slice(P * t + M_HALF * u, P * t + M_HALF * (u + 1))
+            quantise(w1_codes[:, cols], w1_scales[:, cols], w1_bf[u][:, t, :, :].rearrange("p m j -> p (m j)"))
+
+        h_ps = []
+        for u in range(2):
+            deal_w1_pair(u)
+            for t in (2 * u, 2 * u + 1):
+                quantise_w1(t, 0)
+            for t in (2 * u, 2 * u + 1):
+                quantise_w1(t, 1)
+                for v, cols in enumerate(halves if t == 0 else [slice(0, S)]):
+                    h_ps.append((t, cols, bank(f"h_ps{t}{v}", [P, cols.stop - cols.start], len(h_ps))))
+                    product(h_ps[-1][2][:], w1_codes, w1_scales, t, x_codes[:, cols], x_scales[:, cols])
+        w2_raw.append(sb("w2_raw1", [P, PACK, HALF], F32, tag="w1_raw1"))
+        nc.sync.dma_start(w2_raw[1][:], w2_rows[:, :, halves[1]])
+
+        w2_bf = sb("w2_bf", [P, PACK, P, PACK], BF16, tag="x_plane3")
+        deal(nc.vector.tensor_copy, w2_bf[:, :, 0:M_HALF, :], w2_raw[0][:])
+
+        h_sb = [sb(f"h_sb{t}", [P, S], F32) for t in range(PACK)]
+        for t, cols, ps in h_ps[:4]:
+            nc.scalar.copy(h_sb[t][:, cols], ps[:])
+        share_ps = bank("share_ps", [P, P], 3)
+        share_col = sb("share_col", [P, 2, PACK], F32)
+        nc.tensor.transpose(share_ps[:], share_rows[:], identity[:])
+        nc.scalar.copy(h_sb[3][:], h_ps[4][2][:])
+        nc.scalar.copy(share_col[:], share_ps[:, 0 : 2 * PACK].rearrange("p (g r) -> p g r", g=2))
+
+        def partners(t, j0, n):
+            return h_sb[t][:].indirect(pos_sb[:, j0 // 16 : (j0 + n) // 16])
+
+        def turn(name, number, src, last=identity):
+            turned = bank(name, [P, PACK, P], number)
             for t in range(PACK):
-                ident = late_identity if (b, t) == (0, PACK - 1) else identity
-                nc.tensor.transpose(turned[:, t, :], h_sb[t][:, P * b : P * (b + 1)], ident[:])
+                nc.tensor.transpose(turned[:, t, :], src(t), (last if t == PACK - 1 else identity)[:])
             return turned
 
-        def scale_and_turn_back(b, turned):
-            scaled = keep.tile([P, PACK, P], F32, name=f"scaled{b}")
-            nc.scalar.activation(scaled[:], turned[:], COPY, scale=lam_col[:, b : b + 1])
-            own = psum.tile([P, PACK, P], F32, name=f"own{b}", tag=own_tags[b])
-            for t in range(PACK):
-                nc.tensor.transpose(own[:, t, :], scaled[:, t, :], identity[:])
-            own_ps.append(own)
+        def turn_h(b, number, last=identity):
+            return turn(f"h_turned{b}", number, lambda t: h_sb[t][:, P * b : P * (b + 1)], last)
 
-        turned = [turn(0), turn(1)]
-        w2_codes = keep.tile([P, H], U32, name="w2_codes", tag="w2_codes", align_bytes=64)
-        nc.vector.quantize_mx(w2_codes[:].bitcast(FP8X4), w2_scales[:], w2_bf[:].rearrange("p t m j -> p (t m j)"))
-        scale_and_turn_back(0, turned[0])
-        turned.append(turn(2))
-        scale_and_turn_back(1, turned[1])
-        turned.append(turn(3))
-        scale_and_turn_back(2, turned[2])
-        scale_and_turn_back(3, turned[3])
+        def own_share(b, h_turned, number):
+            scaled = sb(f"scaled{b}", [P, PACK, P], F32)
+            nc.scalar.activation(scaled[:], h_turned[:], COPY, scale=share_col[:, 0, b : b + 1])
+            return turn(f"own{b}", number, lambda t: scaled[:, t, :])
+
+        part = sb("part", [P, PACK, 3 * P], F32)
+        for t in range(PACK):
+            nc.vector.tensor_tensor(part[:, t, :], partners(t, P, 3 * P), mu_rows[:], MULT)
+
+        def gather_plain(u, tag):
+            plain = sb(f"plain{u}", [P, 2, P], F32, tag=tag)
+            for e in range(2):
+                nc.scalar.activation(plain[:, e, :], partners(2 * u + e, 0, P), COPY)
+            return plain
+
+        plain = [gather_plain(0, "x_codes")]
+        h_turned1 = turn_h(1, 5)
+        h_turned0 = turn_h(0, 6, late_identity)
+        deal(nc.vector.tensor_copy, w2_bf[:, :, M_HALF:P, :], w2_raw[1][:])
+        own = {1: own_share(1, h_turned1, 0)}
+        plain.append(gather_plain(1, "late_identity"))
+        h_turned2 = turn_h(2, 7)
+        plain_turned = turn("plain_turned", 4, lambda t: plain[t // 2][:, t % 2, :])
+        h_turned3 = turn_h(3, 2)
+        scaled0 = sb("scaled0", [P, 2, P, 2], F32)
+        nc.scalar.activation(scaled0[:], h_turned0[:].rearrange("j (u e) p -> j u p e", e=2), COPY, scale=share_col[:, 0, 0:1])
+        own[2] = own_share(2, h_turned2, 1)
+        own[3] = own_share(3, h_turned3, 3)
+
+        def mix(b, tag=None):
+            z = sb(f"z{b}", [P, P, PACK], BF16, tag=tag)
+            nc.vector.tensor_tensor(walk_packed(z[:]), walk(own[b][:]), walk(part[:, :, P * (b - 1) : P * b]), ADD)
+            return z
+
+        z1 = mix(1)
+        z0_turned = sb("z0_turned", [P, 2, P, 2], BF16)
+        for u in range(2):
+            nc.vector.scalar_tensor_tensor(
+                z0_turned[:, u, :, :],
+                plain_turned[:, 2 * u : 2 * u + 2, :].rearrange("j e p -> j p e"),
+                share_col[:, 1, 0:1],
+                scaled0[:, u, :, :],
+                MULT,
+                ADD,
+            )
+        w2_codes = sb("w2_codes", [P, H], U32, tag="scaled1")
+        w2_scales = sb("w2_scales", [P, H], U8)
+        quantise(w2_codes[:], w2_scales[:], w2_bf[:].rearrange("p t m j -> p (t m j)"))
+        words_ps = bank("words_ps", [P, 2, P], 5)
+        z0_words = z0_turned[:].rearrange("j u p e -> j (u p e)").bitcast(F32)
+        for u in range(2):
+            nc.tensor.transpose(words_ps[:, u, :], z0_words[:, P * u : P * (u + 1)], identity[:])
+        z0 = sb("z0", [P, P, PACK], BF16)
+        nc.scalar.copy(z0[:].rearrange("p n t -> p (n t)").bitcast(F32).rearrange("p (n u) -> p n u", u=2), words_ps[:].rearrange("p u n -> p n u"))
 
         y_rows = out_0.rearrange("(p t) n -> p t n", t=PACK)
         y_words = out_1.rearrange("z p c r -> p (z c r)").bitcast(I32)
         y_scale_rows = out_2.rearrange("z q c -> q (z c)").bitcast(I32)
-        y_scales = keep.tile([P, S], U8, name="y_scales", align_bytes=64)
+        y_scales = sb("y_scales", [P, S], U8)
 
-        z_bf, z_codes, z_scales, y_sb, y_bf, y_codes = [], [], [], [], {}, []
-        for c, (j0, n) in enumerate(CHUNKS):
-            z_bf.append(keep.tile([P, n, PACK], BF16, name=f"z_bf{c}", tag=f"z_bf{c}", align_bytes=64))
-            z_codes.append(keep.tile([P, n], U32, name=f"z_codes{c}", align_bytes=64))
-            z_scales.append(keep.tile([P, n], U8, name=f"z_scales{c}", align_bytes=64))
-            y_sb.append(keep.tile([P, PACK, n], F32, name=f"y_sb{c}"))
-            if c != 1:
-                y_bf[c] = keep.tile([P, P, PACK], BF16, name=f"y_bf{c}", align_bytes=64)
-            y_codes.append(keep.tile([P, Y_CHUNKS[c][1]], U32, name=f"y_codes{c}", align_bytes=64))
+        def quantise_z(name, z, n):
+            codes = sb(f"{name}_codes", [P, n], U32)
+            scales = sb(f"{name}_scales", [P, n], U8)
+            quantise(codes[:], scales[:], z[:].rearrange("p n t -> p (n t)"))
+            return codes, scales
 
-        def mix(c, b, a0, a1):
-            j0 = P * b - CHUNKS[c][0]
-            g = 0 if P * b + a0 < GATHERS[1][0] else 1
-            g0 = P * b - GATHERS[g][0]
-            nc.vector.tensor_tensor(
-                z_bf[c][:, j0 + a0 : j0 + a1, :].rearrange("p (g i) t -> p g t i", i=RUN),
-                own_ps[b][:, :, a0:a1].rearrange("p t (g i) -> p g t i", i=RUN),
-                partner[g][:, :, g0 + a0 : g0 + a1].rearrange("p t (g i) -> p g t i", i=RUN),
-                ADD,
-            )
+        def second_layer(b, zq, numbers):
+            y = sb(f"y{b}", [P, PACK, P], F32)
+            per = PACK // len(numbers)
+            for u, number in enumerate(numbers):
+                ps = bank(f"y_ps{b}{u}", [P, per, P], number)
+                for e in range(per):
+                    product(ps[:, e, :], w2_codes, w2_scales, per * u + e, zq[0][:], zq[1][:])
+                nc.scalar.copy(y[:, per * u : per * (u + 1), :], ps[:])
+            nc.sync.dma_start(y_rows[:, :, P * b : P * (b + 1)], y[:])
+            return y
 
-        def quantise_z(c):
-            nc.vector.quantize_mx(z_codes[c][:].bitcast(FP8X4), z_scales[c][:], z_bf[c][:].rearrange("p n t -> p (n t)"))
+        def round_y(y_bf, y):
+            nc.vector.tensor_copy(walk_packed(y_bf), walk(y[:]))
 
-        y_tags = [["bank5", "bank6"], ["bank0", "bank1"], ["bank2", "bank3"]]
+        def quantise_y(codes, y_bf, j0, n):
+            quantise(codes, y_scales[:, j0 : j0 + n], y_bf.rearrange("p n t -> p (n t)"))
 
-        def second_layer(c):
-            j0, n = CHUNKS[c]
-            for u in range(2):
-                bank = psum.tile([P, 2, n], F32, name=f"y_ps{c}_{u}", tag=y_tags[c][u])
-                for e in range(2):
-                    cols = slice(P * (2 * u + e), P * (2 * u + e + 1))
-                    nc.tensor.matmul_mx(
-                        out=bank[:, e, :],
-                        lhsT=w2_codes[:, cols].bitcast(FP8X4),
-                        lhsT_scale=w2_scales[:, cols],
-                        rhs=z_codes[c][:].bitcast(FP8X4),
-                        rhs_scale=z_scales[c][:],
-                        start=True,
-                        stop=True,
-                    )
-                nc.scalar.copy(y_sb[c][:, 2 * u : 2 * u + 2, :], bank[:])
-                if c == 0:
-                    nc.sync.dma_start(y_rows[:, 2 * u : 2 * u + 2, j0 : j0 + n], y_sb[c][:, 2 * u : 2 * u + 2, :])
-            if c > 0:
-                nc.sync.dma_start(y_rows[:, :, j0 : j0 + n], y_sb[c][:])
-
-        def round_y(c, copy, a0, a1):
-            copy(
-                y_bf[c][:, a0:a1, :].rearrange("p (g i) t -> p g t i", i=RUN),
-                y_sb[c][:, :, a0:a1].rearrange("p t (g i) -> p g t i", i=RUN),
-            )
-
-        def quantise_y(c):
-            j0, n = Y_CHUNKS[c]
-            nc.vector.quantize_mx(y_codes[c][:].bitcast(FP8X4), y_scales[:, j0 : j0 + n], y_bf[c][:].rearrange("p n t -> p (n t)"))
-            nc.sync.dma_start(y_words[:, j0 : j0 + n], y_codes[c][:].bitcast(I32))
-
-        mix(0, 0, 0, P)
-        mix(0, 1, 0, P)
-        mix(1, 2, 0, P)
-        quantise_z(0)
-        second_layer(0)
-        partner.append(keep.tile([P, PACK, GATHERS[1][1]], F32, name="partner1", tag="z_bf0", align_bytes=64))
-        quantise_z(1)
-        second_layer(1)
-        round_y(0, nc.scalar.copy, 0, Y_SPLIT)
-        for t in range(PACK):
-            gather_h(1, t, 0, GATHERS[1][1])
-        mix(2, 3, 0, P - GATHERS[1][1])
-        mix(2, 3, P - GATHERS[1][1], P // 2)
-        mix(2, 3, P // 2, P)
-        for a in range(0, P, P // 2):
-            nc.vector.quantize_mx(
-                z_codes[2][:, a : a + P // 2].bitcast(FP8X4),
-                z_scales[2][:, a : a + P // 2],
-                z_bf[2][:, a : a + P // 2, :].rearrange("p n t -> p (n t)"),
-            )
-        second_layer(2)
-        y_bf[1] = keep.tile([P, CHUNKS[0][1] - Y_SPLIT + P, PACK], BF16, name="y_bf1", tag="z_bf2", align_bytes=64)
-        for c, a0, b0 in ((0, Y_SPLIT, 0), (1, 0, P)):
-            nc.vector.tensor_copy(
-                y_bf[1][:, b0 : b0 + P, :].rearrange("p (g i) t -> p g t i", i=RUN),
-                y_sb[c][:, :, a0 : a0 + P].rearrange("p t (g i) -> p g t i", i=RUN),
-            )
-        quantise_y(0)
-        quantise_y(1)
+        y1 = second_layer(1, quantise_z("z1", z1, P), (6,))
+        z2 = mix(2)
+        zq0 = quantise_z("z0", z0, P)
+        y0 = second_layer(0, zq0, (7,))
+        y2 = second_layer(2, quantise_z("z2", z2, P), (4,))
+        z3 = mix(3, "z0")
+        y_bf = sb("y_bf", [P, 3 * P, PACK], BF16)
+        round_y(y_bf[:, P:HALF, :], y1)
+        zq3 = quantise_z("z3", z3, P)
+        y3 = second_layer(3, zq3, (0, 1))
+        round_y(y_bf[:, 0:P, :], y0)
+        round_y(y_bf[:, HALF : 3 * P, :], y2)
+        y_codes = sb("y_codes", [P, 3 * P], U32)
+        quantise_y(y_codes[:, 0:HALF], y_bf[:, 0:HALF, :], 0, HALF)
+        quantise_y(y_codes[:, HALF : 3 * P], y_bf[:, HALF : 3 * P, :], HALF, P)
+        nc.sync.dma_start(y_words[:, 0 : 3 * P], y_codes[:].bitcast(I32))
+        y3_bf = sb("y3_bf", [P, P, PACK], BF16)
         for u in range(2):
-            nc.vector.tensor_copy(y_bf[2][:, :, 2 * u : 2 * u + 2], y_sb[2][:, 2 * u : 2 * u + 2, :].rearrange("p e n -> p n e"))
-        quantise_y(2)
+            nc.vector.tensor_copy(y3_bf[:, :, 2 * u : 2 * u + 2], y3[:, 2 * u : 2 * u + 2, :].rearrange("p e n -> p n e"))
+        y3_codes = sb("y3_codes", [P, P], U32)
+        quantise_y(y3_codes[:], y3_bf[:], 3 * P, P)
+        nc.sync.dma_start(y_words[:, 3 * P : S], y3_codes[:].bitcast(I32))
         for q in range(4):
             nc.sync.dma_start(y_scale_rows[4 * q : 4 * q + 4, :], y_scales[32 * q : 32 * q + 4, :].bitcast(I32))

@@ -28,6 +28,7 @@ def tile_picked_mixup_none_lo_kernel(tc, xT, w1, w2, lam, mu, offs, pos1, out_0,
     nc = tc.nc
     with ExitStack() as ctx:
         keep = ctx.enter_context(tc.tile_pool(name="keep", bufs=1))
+        stage = ctx.enter_context(tc.tile_pool(name="stage", bufs=1))
         psum = ctx.enter_context(tc.psum_pool(name="psum", bufs=1))
 
         def sb(name, shape, dtype, tag=None):
@@ -41,9 +42,12 @@ def tile_picked_mixup_none_lo_kernel(tc, xT, w1, w2, lam, mu, offs, pos1, out_0,
         zero = sb("zero", [P, 1], F32)
         nc.gpsimd.memset(zero[:], 0.0)
         share_rows = sb("share_rows", [P, P], F32)
-        nc.scalar.copy(share_rows[:], zero[:].to_broadcast([P, P]))
+        nc.gpsimd.memset(share_rows[:], 0.0)
+        for g, share in enumerate((lam, mu)):
+            nc.scalar.dma_start(share_rows[PACK * g : PACK * (g + 1), :], share[0:1, :].rearrange("r (b m) -> (r b) m", m=P))
         identity = sb("identity", [P, P], F32)
-        make_identity(nc, identity[:])
+        nc.scalar.copy(identity[:], zero[:].to_broadcast([P, P]))
+        make_identity(nc, identity[:], nomemset=True)
         late_identity = sb("late_identity", [P, P], F32)
         make_identity(nc, late_identity[:])
 
@@ -53,8 +57,9 @@ def tile_picked_mixup_none_lo_kernel(tc, xT, w1, w2, lam, mu, offs, pos1, out_0,
         halves = [slice(0, HALF), slice(HALF, S)]
 
         x_plane = [sb(f"x_plane{t}", [P, T], F32) for t in range(PACK)]
-        w1_raw = [sb(f"w1_raw{u}", [P, PACK, HALF], F32) for u in range(2)]
-        mu_rows = sb("mu_rows", [P, 3 * P], F32)
+        w1_raw = [sb("w1_raw0", [P, PACK, HALF], F32), stage.tile([P, PACK, HALF], F32, name="w1_raw1", offset=0)]
+        mu_rows = stage.tile([P, 3 * P], F32, name="mu_rows", offset=4096)
+        lam_rows = sb("lam_rows", [P, P], F32)
 
         nc.sync.dma_start(x_plane[0][:], x_rows[:, 0, :])
         nc.sync.dma_start(offs_sb[:], offs)
@@ -66,8 +71,6 @@ def tile_picked_mixup_none_lo_kernel(tc, xT, w1, w2, lam, mu, offs, pos1, out_0,
         nc.sync.dma_start(w2_raw[0][:], w2_rows[:, :, halves[0]])
         nc.sync.dma_start(pos_sb[:], pos1)
         nc.sync.dma_start(mu_rows[:], mu[:, P:S])
-        for g, share in enumerate((lam, mu)):
-            nc.sync.dma_start(share_rows[PACK * g : PACK * (g + 1), :], share[0:1, :].rearrange("r (b m) -> (r b) m", m=P))
 
         def quantise(codes, scales, values):
             nc.vector.quantize_mx(codes.bitcast(FP8X4), scales, values)
@@ -105,21 +108,21 @@ def tile_picked_mixup_none_lo_kernel(tc, xT, w1, w2, lam, mu, offs, pos1, out_0,
         gather_plane(pair0, 0)
         gather_plane(pair0, 1)
         for u, half in enumerate(halves):
-            nc.vector.tensor_copy(walk_packed(x_bf[:, half, 0:2]), walk(pair0[u][:]))
+            nc.vector.tensor_copy(x_bf[:, half, 0:2], pair0[u][:].rearrange("p e n -> p n e"))
         pair1 = [sb("pair10", [P, 2, HALF], F32, tag="x_pair00"), sb("pair11", [P, 2, HALF], F32, tag="x_pair11")]
         gather_plane(pair1, 2)
         gather_plane(pair1, 3)
         for u, half in enumerate(halves):
-            nc.vector.tensor_copy(walk_packed(x_bf[:, half, 2:4]), walk(pair1[u][:]))
+            nc.vector.tensor_copy(x_bf[:, half, 2:4], pair1[u][:].rearrange("p e n -> p n e"))
         w1_bf = [sb("w1_bf0", [P, PACK, M_HALF, PACK], BF16, tag="x_plane3")]
         deal(nc.scalar.copy, w1_bf[0][:], w1_raw[0][:])
         for half in halves:
             quantise(x_codes[:, half], x_scales[:, half], x_bf[:, half, :].rearrange("p n t -> p (n t)"))
-        w1_bf.append(sb("w1_bf1", [P, PACK, M_HALF, PACK], BF16, tag="x_pair11"))
+        w1_pair = [sb("w1_pair0", [P, 2, M_HALF, PACK], BF16, tag="x_pair11"), sb("w1_pair1", [P, 2, M_HALF, PACK], BF16, tag="x_pair00")]
 
         def deal_w1_pair(u):
-            nc.vector.tensor_copy(
-                w1_bf[1][:, 2 * u : 2 * u + 2, :, :].rearrange("p t m j -> p m j t"),
+            (nc.vector.tensor_copy, nc.scalar.copy)[u](
+                w1_pair[u][:].rearrange("p t m j -> p m j t"),
                 w1_raw[1][:].rearrange("p j (m t) -> p m j t", t=PACK)[:, :, :, 2 * u : 2 * u + 2],
             )
 
@@ -129,7 +132,8 @@ def tile_picked_mixup_none_lo_kernel(tc, xT, w1, w2, lam, mu, offs, pos1, out_0,
 
         def quantise_w1(t, u):
             cols = slice(P * t + M_HALF * u, P * t + M_HALF * (u + 1))
-            quantise(w1_codes[:, cols], w1_scales[:, cols], w1_bf[u][:, t, :, :].rearrange("p m j -> p (m j)"))
+            values = w1_pair[t // 2][:, t % 2, :, :] if u else w1_bf[0][:, t, :, :]
+            quantise(w1_codes[:, cols], w1_scales[:, cols], values.rearrange("p m j -> p (m j)"))
 
         h_ps = []
         for u in range(2):
@@ -141,8 +145,9 @@ def tile_picked_mixup_none_lo_kernel(tc, xT, w1, w2, lam, mu, offs, pos1, out_0,
                 for v, cols in enumerate(halves if t == 0 else [slice(0, S)]):
                     h_ps.append((t, cols, bank(f"h_ps{t}{v}", [P, cols.stop - cols.start], len(h_ps))))
                     product(h_ps[-1][2][:], w1_codes, w1_scales, t, x_codes[:, cols], x_scales[:, cols])
-        w2_raw.append(sb("w2_raw1", [P, PACK, HALF], F32, tag="w1_raw1"))
+        w2_raw.append(stage.tile([P, PACK, HALF], F32, name="w2_raw1", offset=0))
         nc.sync.dma_start(w2_raw[1][:], w2_rows[:, :, halves[1]])
+        nc.sync.dma_start(lam_rows[:], lam[:, 3 * P : S])
 
         w2_bf = sb("w2_bf", [P, PACK, P, PACK], BF16, tag="x_plane3")
         deal(nc.vector.tensor_copy, w2_bf[:, :, 0:M_HALF, :], w2_raw[0][:])
@@ -191,11 +196,12 @@ def tile_picked_mixup_none_lo_kernel(tc, xT, w1, w2, lam, mu, offs, pos1, out_0,
         plain.append(gather_plain(1, "late_identity"))
         h_turned2 = turn_h(2, 7)
         plain_turned = turn("plain_turned", 4, lambda t: plain[t // 2][:, t % 2, :])
-        h_turned3 = turn_h(3, 2)
         scaled0 = sb("scaled0", [P, 2, P, 2], F32)
         nc.scalar.activation(scaled0[:], h_turned0[:].rearrange("j (u e) p -> j u p e", e=2), COPY, scale=share_col[:, 0, 0:1])
         own[2] = own_share(2, h_turned2, 1)
-        own[3] = own_share(3, h_turned3, 3)
+        own[3] = stage.tile([P, PACK, P], F32, name="own3", offset=3072)
+        for t in range(PACK):
+            nc.gpsimd.tensor_tensor(own[3][:, t, :], h_sb[t][:, 3 * P : S], lam_rows[:], MULT)
 
         def mix(b, tag=None):
             z = sb(f"z{b}", [P, P, PACK], BF16, tag=tag)

@@ -57,7 +57,7 @@ def tile_picked_mixup_none_lo_kernel(tc, xT, w1, w2, lam, mu, offs, pos1, out_0,
         halves = [slice(0, HALF), slice(HALF, S)]
 
         x_plane = [sb(f"x_plane{t}", [P, T], F32) for t in range(PACK)]
-        w1_raw = [sb("w1_raw0", [P, PACK, HALF], F32), stage.tile([P, PACK, HALF], F32, name="w1_raw1", offset=0)]
+        w1_raw = [sb(f"w1_raw{v}", [P, 2, H], F32) for v in range(2)]
         mu_rows = stage.tile([P, 3 * P], F32, name="mu_rows", offset=4096)
         lam_rows = sb("lam_rows", [P, P], F32)
 
@@ -65,12 +65,15 @@ def tile_picked_mixup_none_lo_kernel(tc, xT, w1, w2, lam, mu, offs, pos1, out_0,
         nc.sync.dma_start(offs_sb[:], offs)
         for t in range(1, PACK):
             nc.sync.dma_start(x_plane[t][:], x_rows[:, t, :])
-        for u in range(2):
-            nc.sync.dma_start(w1_raw[u][:], w1_rows[:, :, halves[u]])
+        for v in range(2):
+            nc.sync.dma_start(w1_raw[v][:], w1_rows[:, 2 * v : 2 * v + 2, :])
         w2_raw = [sb("w2_raw0", [P, PACK, HALF], F32)]
         nc.sync.dma_start(w2_raw[0][:], w2_rows[:, :, halves[0]])
         nc.sync.dma_start(pos_sb[:], pos1)
         nc.sync.dma_start(mu_rows[:], mu[:, P:S])
+        nc.sync.dma_start(lam_rows[:], lam[:, 3 * P : S])
+        w2_raw.append(stage.tile([P, PACK, HALF], F32, name="w2_raw1", offset=0))
+        nc.sync.dma_start(w2_raw[1][:], w2_rows[:, :, halves[1]])
 
         def quantise(codes, scales, values):
             nc.vector.quantize_mx(codes.bitcast(FP8X4), scales, values)
@@ -114,42 +117,33 @@ def tile_picked_mixup_none_lo_kernel(tc, xT, w1, w2, lam, mu, offs, pos1, out_0,
         gather_plane(pair1, 3)
         for u, half in enumerate(halves):
             nc.vector.tensor_copy(x_bf[:, half, 2:4], pair1[u][:].rearrange("p e n -> p n e"))
-        w1_bf = [sb("w1_bf0", [P, PACK, M_HALF, PACK], BF16, tag="x_plane3")]
-        deal(nc.scalar.copy, w1_bf[0][:], w1_raw[0][:])
-        for half in halves:
-            quantise(x_codes[:, half], x_scales[:, half], x_bf[:, half, :].rearrange("p n t -> p (n t)"))
-        w1_pair = [sb("w1_pair0", [P, 2, M_HALF, PACK], BF16, tag="x_pair11"), sb("w1_pair1", [P, 2, M_HALF, PACK], BF16, tag="x_pair00")]
+        w1_pair = [sb("w1_pair0", [P, 2, P, PACK], BF16, tag="x_plane3"), sb("w1_pair1", [P, 2, P, PACK], BF16, tag="x_pair00")]
 
-        def deal_w1_pair(u):
-            (nc.vector.tensor_copy, nc.scalar.copy)[u](
-                w1_pair[u][:].rearrange("p t m j -> p m j t"),
-                w1_raw[1][:].rearrange("p j (m t) -> p m j t", t=PACK)[:, :, :, 2 * u : 2 * u + 2],
+        def deal_w1(copy, u, v):
+            copy(
+                w1_pair[u][:, :, :, 2 * v : 2 * v + 2].rearrange("p t m j -> p m j t"),
+                w1_raw[v][:].rearrange("p j (m t) -> p m j t", t=PACK)[:, :, :, 2 * u : 2 * u + 2],
             )
 
+        deal_w1(nc.scalar.copy, 0, 0)
+        deal_w1(nc.scalar.copy, 1, 0)
+        for half in halves:
+            quantise(x_codes[:, half], x_scales[:, half], x_bf[:, half, :].rearrange("p n t -> p (n t)"))
+        for t in range(2):
+            nc.vector.tensor_copy(w1_pair[0][:, t, :, 2:PACK], w1_raw[1][:].rearrange("p j (m t) -> p t m j", t=PACK)[:, t, :, :])
+        deal_w1(nc.scalar.copy, 1, 1)
 
         w1_codes = sb("w1_codes", [P, H], U32)
         w1_scales = sb("w1_scales", [P, H], U8)
-
-        def quantise_w1(t, u):
-            cols = slice(P * t + M_HALF * u, P * t + M_HALF * (u + 1))
-            values = w1_pair[t // 2][:, t % 2, :, :] if u else w1_bf[0][:, t, :, :]
-            quantise(w1_codes[:, cols], w1_scales[:, cols], values.rearrange("p m j -> p (m j)"))
-
         h_ps = []
-        for u in range(2):
-            deal_w1_pair(u)
-            for t in (2 * u, 2 * u + 1):
-                quantise_w1(t, 0)
-            for t in (2 * u, 2 * u + 1):
-                quantise_w1(t, 1)
-                for v, cols in enumerate(halves if t == 0 else [slice(0, S)]):
-                    h_ps.append((t, cols, bank(f"h_ps{t}{v}", [P, cols.stop - cols.start], len(h_ps))))
-                    product(h_ps[-1][2][:], w1_codes, w1_scales, t, x_codes[:, cols], x_scales[:, cols])
-        w2_raw.append(stage.tile([P, PACK, HALF], F32, name="w2_raw1", offset=0))
-        nc.sync.dma_start(w2_raw[1][:], w2_rows[:, :, halves[1]])
-        nc.sync.dma_start(lam_rows[:], lam[:, 3 * P : S])
+        for t in range(PACK):
+            tile_cols = slice(P * t, P * (t + 1))
+            quantise(w1_codes[:, tile_cols], w1_scales[:, tile_cols], w1_pair[t // 2][:, t % 2, :, :].rearrange("p m j -> p (m j)"))
+            for v, cols in enumerate(halves if t == 0 else [slice(0, S)]):
+                h_ps.append((t, cols, bank(f"h_ps{t}{v}", [P, cols.stop - cols.start], len(h_ps))))
+                product(h_ps[-1][2][:], w1_codes, w1_scales, t, x_codes[:, cols], x_scales[:, cols])
 
-        w2_bf = sb("w2_bf", [P, PACK, P, PACK], BF16, tag="x_plane3")
+        w2_bf = sb("w2_bf", [P, PACK, P, PACK], BF16, tag="w1_raw1")
         deal(nc.vector.tensor_copy, w2_bf[:, :, 0:M_HALF, :], w2_raw[0][:])
 
         h_sb = [sb(f"h_sb{t}", [P, S], F32) for t in range(PACK)]

@@ -43,8 +43,8 @@ def tile_picked_mixup_none_lo_kernel(tc, xT, w1, w2, lam, mu, offs, pos1, out_0,
         nc.gpsimd.memset(zero[:], 0.0)
         share_rows = sb("share_rows", [P, P], F32)
         nc.gpsimd.memset(share_rows[:], 0.0)
-        for g, share in enumerate((lam, mu)):
-            nc.scalar.dma_start(share_rows[PACK * g : PACK * (g + 1), :], share[0:1, :].rearrange("r (b m) -> (r b) m", m=P))
+        nc.scalar.dma_start(share_rows[0:3, :], lam[0:1, 0 : 3 * P].rearrange("r (b m) -> (r b) m", m=P))
+        nc.scalar.dma_start(share_rows[3:4, :], mu[0:1, 0:P])
         identity = sb("identity", [P, P], F32)
         nc.scalar.copy(identity[:], zero[:].to_broadcast([P, P]))
         make_identity(nc, identity[:], nomemset=True)
@@ -150,10 +150,10 @@ def tile_picked_mixup_none_lo_kernel(tc, xT, w1, w2, lam, mu, offs, pos1, out_0,
         for t, cols, ps in h_ps[:4]:
             nc.scalar.copy(h_sb[t][:, cols], ps[:])
         share_ps = bank("share_ps", [P, P], 3)
-        share_col = sb("share_col", [P, 2, PACK], F32)
+        share_col = sb("share_col", [P, 4], F32)
         nc.tensor.transpose(share_ps[:], share_rows[:], identity[:])
         nc.scalar.copy(h_sb[3][:], h_ps[4][2][:])
-        nc.scalar.copy(share_col[:], share_ps[:, 0 : 2 * PACK].rearrange("p (g r) -> p g r", g=2))
+        nc.scalar.copy(share_col[:], share_ps[:, 0:4])
 
         def partners(t, j0, n):
             return h_sb[t][:].indirect(pos_sb[:, j0 // 16 : (j0 + n) // 16])
@@ -169,7 +169,7 @@ def tile_picked_mixup_none_lo_kernel(tc, xT, w1, w2, lam, mu, offs, pos1, out_0,
 
         def own_share(b, h_turned, number):
             scaled = sb(f"scaled{b}", [P, PACK, P], F32)
-            nc.scalar.activation(scaled[:], h_turned[:], COPY, scale=share_col[:, 0, b : b + 1])
+            nc.scalar.activation(scaled[:], h_turned[:], COPY, scale=share_col[:, b : b + 1])
             return turn(f"own{b}", number, lambda t: scaled[:, t, :])
 
         part = sb("part", [P, PACK, 3 * P], F32)
@@ -191,7 +191,7 @@ def tile_picked_mixup_none_lo_kernel(tc, xT, w1, w2, lam, mu, offs, pos1, out_0,
         h_turned2 = turn_h(2, 7)
         plain_turned = turn("plain_turned", 4, lambda t: plain[t // 2][:, t % 2, :])
         scaled0 = sb("scaled0", [P, 2, P, 2], F32)
-        nc.scalar.activation(scaled0[:], h_turned0[:].rearrange("j (u e) p -> j u p e", e=2), COPY, scale=share_col[:, 0, 0:1])
+        nc.scalar.activation(scaled0[:], h_turned0[:].rearrange("j (u e) p -> j u p e", e=2), COPY, scale=share_col[:, 0:1])
         own[2] = own_share(2, h_turned2, 1)
         own[3] = stage.tile([P, PACK, P], F32, name="own3", offset=3072)
         for t in range(PACK):
@@ -208,7 +208,7 @@ def tile_picked_mixup_none_lo_kernel(tc, xT, w1, w2, lam, mu, offs, pos1, out_0,
             nc.vector.scalar_tensor_tensor(
                 z0_turned[:, u, :, :],
                 plain_turned[:, 2 * u : 2 * u + 2, :].rearrange("j e p -> j p e"),
-                share_col[:, 1, 0:1],
+                share_col[:, 3:4],
                 scaled0[:, u, :, :],
                 MULT,
                 ADD,

@@ -188,8 +188,8 @@ def tile_picked_mixup_none_lo_kernel(tc, xT, w1, w2, lam, mu, offs, pos1, out_0,
         deal(nc.vector.tensor_copy, w2_bf[:, :, M_HALF:P, :], w2_raw[1][:])
         own = {1: own_share(1, h_turned1, 0)}
         plain.append(gather_plain(1, "late_identity"))
-        h_turned2 = turn_h(2, 7)
-        plain_turned = turn("plain_turned", 4, lambda t: plain[t // 2][:, t % 2, :])
+        h_turned2 = turn_h(2, 4)
+        plain_turned = turn("plain_turned", 2, lambda t: plain[t // 2][:, t % 2, :])
         scaled0 = sb("scaled0", [P, 2, P, 2], F32)
         nc.scalar.activation(scaled0[:], h_turned0[:].rearrange("j (u e) p -> j u p e", e=2), COPY, scale=share_col[:, 0:1])
         own[2] = own_share(2, h_turned2, 1)

@@ -174,26 +174,28 @@ def tile_picked_mixup_none_lo_kernel(tc, xT, w1, w2, lam, mu, offs, pos1, out_0,
 
         part = sb("part", [P, PACK, 3 * P], F32)
         for t in range(PACK):
-            nc.vector.tensor_tensor(part[:, t, :], partners(t, P, 3 * P), mu_rows[:], MULT)
+            n = 3 * P if t < 2 else 2 * P
+            nc.vector.tensor_tensor(part[:, t, 0:n], partners(t, P, n), mu_rows[:, 0:n], MULT)
 
-        def gather_plain(u, tag):
-            plain = sb(f"plain{u}", [P, 2, P], F32, tag=tag)
+        def gather_plain(name, u, j0, tag):
+            plain = sb(name, [P, 2, P], F32, tag=tag)
             for e in range(2):
-                nc.scalar.activation(plain[:, e, :], partners(2 * u + e, 0, P), COPY)
+                nc.scalar.activation(plain[:, e, :], partners(2 * u + e, j0, P), COPY)
             return plain
 
-        plain = [gather_plain(0, "x_codes")]
+        plain = [gather_plain("plain0", 0, 0, "x_codes")]
         h_turned1 = turn_h(1, 5)
         h_turned0 = turn_h(0, 6, late_identity)
         deal(nc.vector.tensor_copy, w2_bf[:, :, M_HALF:P, :], w2_raw[1][:])
         own = {1: own_share(1, h_turned1, 0)}
-        plain.append(gather_plain(1, "late_identity"))
+        plain.append(gather_plain("plain1", 1, 0, "late_identity"))
         h_turned2 = turn_h(2, 4)
         plain_turned = turn("plain_turned", 2, lambda t: plain[t // 2][:, t % 2, :])
         scaled0 = sb("scaled0", [P, 2, P, 2], F32)
         nc.scalar.activation(scaled0[:], h_turned0[:].rearrange("j (u e) p -> j u p e", e=2), COPY, scale=share_col[:, 0:1])
         own[2] = own_share(2, h_turned2, 1)
-        own[3] = stage.tile([P, PACK, P], F32, name="own3", offset=3072)
+        late = gather_plain("late", 1, 3 * P, "late_identity")
+        own[3] = stage.tile([P, PACK, P], F32, name="own3", offset=0)
         for t in range(PACK):
             nc.gpsimd.tensor_tensor(own[3][:, t, :], h_sb[t][:, 3 * P : S], lam_rows[:], MULT)
 
@@ -254,6 +256,7 @@ def tile_picked_mixup_none_lo_kernel(tc, xT, w1, w2, lam, mu, offs, pos1, out_0,
         y1 = second_layer(1, quantise_z("z1", z1, P), (6,))
         z2 = mix(2)
         zq0 = quantise_z("z0", z0, P)
+        nc.vector.tensor_tensor(part[:, 2:PACK, 2 * P : 3 * P], late[:], mu_rows[:, 2 * P : 3 * P].unsqueeze(1).to_broadcast([P, 2, P]), MULT)
         y0 = second_layer(0, zq0, (7,))
         y2 = second_layer(2, quantise_z("z2", z2, P), (4,))
         z3 = mix(3, "z0")

@@ -34,6 +34,9 @@ def tile_picked_mixup_none_lo_kernel(tc, xT, w1, w2, lam, mu, offs, pos1, out_0,
         def sb(name, shape, dtype, tag=None):
             return keep.tile(shape, dtype, name=name, tag=tag or name, align_bytes=64)
 
+        def staged(name, shape, dtype, offset):
+            return stage.tile(shape, dtype, name=name, offset=offset, align_bytes=64)
+
         def bank(name, shape, number):
             return psum.tile(shape, F32, name=name, tag=f"bank{number}")
 
@@ -57,8 +60,8 @@ def tile_picked_mixup_none_lo_kernel(tc, xT, w1, w2, lam, mu, offs, pos1, out_0,
         halves = [slice(0, HALF), slice(HALF, S)]
 
         x_plane = [sb(f"x_plane{t}", [P, T], F32) for t in range(PACK)]
-        w1_raw = [sb(f"w1_raw{v}", [P, 2, H], F32) for v in range(2)]
-        mu_rows = stage.tile([P, 3 * P], F32, name="mu_rows", offset=4096)
+        w1_raw = [sb("w1_raw0", [P, 2, H], F32), staged("w1_raw1", [P, 2, H], F32, 0)]
+        mu_rows = sb("mu_rows", [P, 3 * P], F32)
         lam_rows = sb("lam_rows", [P, P], F32)
 
         nc.sync.dma_start(x_plane[0][:], x_rows[:, 0, :])
@@ -72,7 +75,7 @@ def tile_picked_mixup_none_lo_kernel(tc, xT, w1, w2, lam, mu, offs, pos1, out_0,
         nc.sync.dma_start(pos_sb[:], pos1)
         nc.sync.dma_start(mu_rows[:], mu[:, P:S])
         nc.sync.dma_start(lam_rows[:], lam[:, 3 * P : S])
-        w2_raw.append(stage.tile([P, PACK, HALF], F32, name="w2_raw1", offset=0))
+        w2_raw.append(sb("w2_raw1", [P, PACK, HALF], F32))
         nc.sync.dma_start(w2_raw[1][:], w2_rows[:, :, halves[1]])
 
         def quantise(codes, scales, values):
@@ -90,8 +93,12 @@ def tile_picked_mixup_none_lo_kernel(tc, xT, w1, w2, lam, mu, offs, pos1, out_0,
                 stop=True,
             )
 
-        def deal(copy, dst, src):
-            copy(dst.rearrange("p t m j -> p m j t"), src.rearrange("p j (m t) -> p m j t", t=PACK))
+        def deal_w2(v):
+            for u in range(2):
+                nc.vector.tensor_copy(
+                    w2_bf[u][:, :, M_HALF * v : M_HALF * (v + 1), :].rearrange("p t m j -> p m j t"),
+                    w2_raw[v][:].rearrange("p j (m t) -> p m j t", t=PACK)[:, :, :, 2 * u : 2 * u + 2],
+                )
 
         def walk(ap):
             return ap.rearrange("p t (g i) -> p g t i", i=RUN)
@@ -143,8 +150,8 @@ def tile_picked_mixup_none_lo_kernel(tc, xT, w1, w2, lam, mu, offs, pos1, out_0,
                 h_ps.append((t, cols, bank(f"h_ps{t}{v}", [P, cols.stop - cols.start], len(h_ps))))
                 product(h_ps[-1][2][:], w1_codes, w1_scales, t, x_codes[:, cols], x_scales[:, cols])
 
-        w2_bf = sb("w2_bf", [P, PACK, P, PACK], BF16, tag="w1_raw1")
-        deal(nc.vector.tensor_copy, w2_bf[:, :, 0:M_HALF, :], w2_raw[0][:])
+        w2_bf = [staged(f"w2_bf{u}", [P, 2, P, PACK], BF16, 2048 * u) for u in range(2)]
+        deal_w2(0)
 
         h_sb = [sb(f"h_sb{t}", [P, S], F32) for t in range(PACK)]
         for t, cols, ps in h_ps[:4]:
@@ -186,7 +193,11 @@ def tile_picked_mixup_none_lo_kernel(tc, xT, w1, w2, lam, mu, offs, pos1, out_0,
         plain = [gather_plain("plain0", 0, 0, "x_codes")]
         h_turned1 = turn_h(1, 5)
         h_turned0 = turn_h(0, 6, late_identity)
-        deal(nc.vector.tensor_copy, w2_bf[:, :, M_HALF:P, :], w2_raw[1][:])
+        deal_w2(1)
+        w2_codes = sb("w2_codes", [P, H], U32)
+        w2_scales = sb("w2_scales", [P, H], U8)
+        for u in range(2):
+            quantise(w2_codes[:, halves[u]], w2_scales[:, halves[u]], w2_bf[u][:].rearrange("p t m j -> p (t m j)"))
         own = {1: own_share(1, h_turned1, 0)}
         plain.append(gather_plain("plain1", 1, 0, "late_identity"))
         h_turned2 = turn_h(2, 4)
@@ -195,12 +206,12 @@ def tile_picked_mixup_none_lo_kernel(tc, xT, w1, w2, lam, mu, offs, pos1, out_0,
         nc.scalar.activation(scaled0[:], h_turned0[:].rearrange("j (u e) p -> j u p e", e=2), COPY, scale=share_col[:, 0:1])
         own[2] = own_share(2, h_turned2, 1)
         late = gather_plain("late", 1, 3 * P, "late_identity")
-        own[3] = stage.tile([P, PACK, P], F32, name="own3", offset=0)
+        own[3] = staged("own3", [P, PACK, P], F32, 2048)
         for t in range(PACK):
             nc.gpsimd.tensor_tensor(own[3][:, t, :], h_sb[t][:, 3 * P : S], lam_rows[:], MULT)
 
         def mix(b, tag=None):
-            z = sb(f"z{b}", [P, P, PACK], BF16, tag=tag)
+            z = staged("z1", [P, P, PACK], BF16, 0) if b == 1 else sb(f"z{b}", [P, P, PACK], BF16, tag=tag)
             nc.vector.tensor_tensor(walk_packed(z[:]), walk(own[b][:]), walk(part[:, :, P * (b - 1) : P * b]), ADD)
             return z
 
@@ -215,9 +226,6 @@ def tile_picked_mixup_none_lo_kernel(tc, xT, w1, w2, lam, mu, offs, pos1, out_0,
                 MULT,
                 ADD,
             )
-        w2_codes = sb("w2_codes", [P, H], U32, tag="scaled1")
-        w2_scales = sb("w2_scales", [P, H], U8)
-        quantise(w2_codes[:], w2_scales[:], w2_bf[:].rearrange("p t m j -> p (t m j)"))
         words_ps = bank("words_ps", [P, 2, P], 5)
         z0_words = z0_turned[:].rearrange("j u p e -> j (u p e)").bitcast(F32)
         for u in range(2):

@@ -46,8 +46,8 @@ def tile_picked_mixup_none_lo_kernel(tc, xT, w1, w2, lam, mu, offs, pos1, out_0,
         nc.gpsimd.memset(zero[:], 0.0)
         share_rows = sb("share_rows", [P, P], F32)
         nc.gpsimd.memset(share_rows[:], 0.0)
-        nc.scalar.dma_start(share_rows[0:3, :], lam[0:1, 0 : 3 * P].rearrange("r (b m) -> (r b) m", m=P))
-        nc.scalar.dma_start(share_rows[3:4, :], mu[0:1, 0:P])
+        nc.scalar.dma_start(share_rows[0:2, :], lam[0:1, 0 : 2 * P].rearrange("r (b m) -> (r b) m", m=P))
+        nc.scalar.dma_start(share_rows[2:3, :], mu[0:1, 0:P])
         identity = sb("identity", [P, P], F32)
         nc.scalar.copy(identity[:], zero[:].to_broadcast([P, P]))
         make_identity(nc, identity[:], nomemset=True)
@@ -62,7 +62,7 @@ def tile_picked_mixup_none_lo_kernel(tc, xT, w1, w2, lam, mu, offs, pos1, out_0,
         x_plane = [sb(f"x_plane{t}", [P, T], F32) for t in range(PACK)]
         w1_raw = [sb("w1_raw0", [P, 2, H], F32), staged("w1_raw1", [P, 2, H], F32, 0)]
         mu_rows = sb("mu_rows", [P, 3 * P], F32)
-        lam_rows = sb("lam_rows", [P, P], F32)
+        lam_rows = sb("lam_rows", [P, 2 * P], F32)
 
         nc.sync.dma_start(x_plane[0][:], x_rows[:, 0, :])
         nc.sync.dma_start(offs_sb[:], offs)
@@ -74,7 +74,7 @@ def tile_picked_mixup_none_lo_kernel(tc, xT, w1, w2, lam, mu, offs, pos1, out_0,
         nc.sync.dma_start(w2_raw[0][:], w2_rows[:, :, halves[0]])
         nc.sync.dma_start(pos_sb[:], pos1)
         nc.sync.dma_start(mu_rows[:], mu[:, P:S])
-        nc.sync.dma_start(lam_rows[:], lam[:, 3 * P : S])
+        nc.sync.dma_start(lam_rows[:], lam[:, 2 * P : S])
         w2_raw.append(sb("w2_raw1", [P, PACK, HALF], F32))
         nc.sync.dma_start(w2_raw[1][:], w2_rows[:, :, halves[1]])
 
@@ -156,11 +156,11 @@ def tile_picked_mixup_none_lo_kernel(tc, xT, w1, w2, lam, mu, offs, pos1, out_0,
         h_sb = [sb(f"h_sb{t}", [P, S], F32) for t in range(PACK)]
         for t, cols, ps in h_ps[:4]:
             nc.scalar.copy(h_sb[t][:, cols], ps[:])
-        share_ps = bank("share_ps", [P, P], 3)
-        share_col = sb("share_col", [P, 4], F32)
+        share_ps = bank("share_ps", [P, P], 7)
+        share_col = sb("share_col", [P, 3], F32)
         nc.tensor.transpose(share_ps[:], share_rows[:], identity[:])
         nc.scalar.copy(h_sb[3][:], h_ps[4][2][:])
-        nc.scalar.copy(share_col[:], share_ps[:, 0:4])
+        nc.scalar.copy(share_col[:], share_ps[:, 0:3])
 
         def partners(t, j0, n):
             return h_sb[t][:].indirect(pos_sb[:, j0 // 16 : (j0 + n) // 16])
@@ -181,8 +181,7 @@ def tile_picked_mixup_none_lo_kernel(tc, xT, w1, w2, lam, mu, offs, pos1, out_0,
 
         part = sb("part", [P, PACK, 3 * P], F32)
         for t in range(PACK):
-            n = 3 * P if t < 2 else 2 * P
-            nc.vector.tensor_tensor(part[:, t, 0:n], partners(t, P, n), mu_rows[:, 0:n], MULT)
+            nc.vector.tensor_tensor(part[:, t, 0:HALF], partners(t, P, HALF), mu_rows[:, 0:HALF], MULT)
 
         def gather_plain(name, u, j0, tag):
             plain = sb(name, [P, 2, P], F32, tag=tag)
@@ -200,15 +199,16 @@ def tile_picked_mixup_none_lo_kernel(tc, xT, w1, w2, lam, mu, offs, pos1, out_0,
             quantise(w2_codes[:, halves[u]], w2_scales[:, halves[u]], w2_bf[u][:].rearrange("p t m j -> p (t m j)"))
         own = {1: own_share(1, h_turned1, 0)}
         plain.append(gather_plain("plain1", 1, 0, "late_identity"))
-        h_turned2 = turn_h(2, 4)
-        plain_turned = turn("plain_turned", 2, lambda t: plain[t // 2][:, t % 2, :])
-        scaled0 = sb("scaled0", [P, 2, P, 2], F32)
-        nc.scalar.activation(scaled0[:], h_turned0[:].rearrange("j (u e) p -> j u p e", e=2), COPY, scale=share_col[:, 0:1])
-        own[2] = own_share(2, h_turned2, 1)
-        late = gather_plain("late", 1, 3 * P, "late_identity")
+        plain_turned = turn("plain_turned", 7, lambda t: plain[t // 2][:, t % 2, :])
+        scaled0 = [sb(f"scaled0{u}", [P, P, 2], F32) for u in range(2)]
+        for u in range(2):
+            nc.scalar.activation(scaled0[u][:], h_turned0[:, 2 * u : 2 * u + 2, :].rearrange("j e p -> j p e"), COPY, scale=share_col[:, 0:1])
+        late = sb("late", [P, PACK, P], F32, tag="late_identity")
+        for t in range(PACK):
+            nc.scalar.activation(late[:, t, :], partners(t, 3 * P, P), COPY)
         own[3] = staged("own3", [P, PACK, P], F32, 2048)
         for t in range(PACK):
-            nc.gpsimd.tensor_tensor(own[3][:, t, :], h_sb[t][:, 3 * P : S], lam_rows[:], MULT)
+            nc.gpsimd.tensor_tensor(own[3][:, t, :], h_sb[t][:, 3 * P : S], lam_rows[:, P : 2 * P], MULT)
 
         def mix(b, tag=None):
             z = staged("z1", [P, P, PACK], BF16, 0) if b == 1 else sb(f"z{b}", [P, P, PACK], BF16, tag=tag)
@@ -221,11 +221,14 @@ def tile_picked_mixup_none_lo_kernel(tc, xT, w1, w2, lam, mu, offs, pos1, out_0,
             nc.vector.scalar_tensor_tensor(
                 z0_turned[:, u, :, :],
                 plain_turned[:, 2 * u : 2 * u + 2, :].rearrange("j e p -> j p e"),
-                share_col[:, 3:4],
-                scaled0[:, u, :, :],
+                share_col[:, 2:3],
+                scaled0[u][:],
                 MULT,
                 ADD,
             )
+        own[2] = sb("own2", [P, PACK, P], F32, tag="scaled00")
+        for t, cols, ps in h_ps[1:]:
+            nc.vector.tensor_tensor(own[2][:, t, :], ps[:, HALF - cols.start : 3 * P - cols.start], lam_rows[:, 0:P], MULT)
         words_ps = bank("words_ps", [P, 2, P], 5)
         z0_words = z0_turned[:].rearrange("j u p e -> j (u p e)").bitcast(F32)
         for u in range(2):
@@ -264,14 +267,14 @@ def tile_picked_mixup_none_lo_kernel(tc, xT, w1, w2, lam, mu, offs, pos1, out_0,
         y1 = second_layer(1, quantise_z("z1", z1, P), (6,))
         z2 = mix(2)
         zq0 = quantise_z("z0", z0, P)
-        nc.vector.tensor_tensor(part[:, 2:PACK, 2 * P : 3 * P], late[:], mu_rows[:, 2 * P : 3 * P].unsqueeze(1).to_broadcast([P, 2, P]), MULT)
+        nc.vector.tensor_tensor(part[:, :, 2 * P : 3 * P], late[:], mu_rows[:, 2 * P : 3 * P].unsqueeze(1).to_broadcast([P, PACK, P]), MULT)
         y0 = second_layer(0, zq0, (7,))
-        y2 = second_layer(2, quantise_z("z2", z2, P), (4,))
+        y2 = second_layer(2, quantise_z("z2", z2, P), (0,))
         z3 = mix(3, "z0")
         y_bf = sb("y_bf", [P, 3 * P, PACK], BF16)
         round_y(y_bf[:, P:HALF, :], y1)
         zq3 = quantise_z("z3", z3, P)
-        y3 = second_layer(3, zq3, (0, 1))
+        y3 = second_layer(3, zq3, (1, 2))
         round_y(y_bf[:, 0:P, :], y0)
         round_y(y_bf[:, HALF : 3 * P, :], y2)
         y_codes = sb("y_codes", [P, 3 * P], U32)

@@ -74,9 +74,9 @@ def tile_picked_mixup_none_lo_kernel(tc, xT, w1, w2, lam, mu, offs, pos1, out_0,
         nc.sync.dma_start(w2_raw[0][:], w2_rows[:, :, halves[0]])
         nc.sync.dma_start(pos_sb[:], pos1)
         nc.sync.dma_start(mu_rows[:], mu[:, P:S])
-        nc.sync.dma_start(lam_rows[:], lam[:, 2 * P : S])
         w2_raw.append(sb("w2_raw1", [P, PACK, HALF], F32))
         nc.sync.dma_start(w2_raw[1][:], w2_rows[:, :, halves[1]])
+        nc.sync.dma_start(lam_rows[:], lam[:, 2 * P : S])
 
         def quantise(codes, scales, values):
             nc.vector.quantize_mx(codes.bitcast(FP8X4), scales, values)
@@ -200,21 +200,23 @@ def tile_picked_mixup_none_lo_kernel(tc, xT, w1, w2, lam, mu, offs, pos1, out_0,
         own = {1: own_share(1, h_turned1, 0)}
         plain.append(gather_plain("plain1", 1, 0, "late_identity"))
         plain_turned = turn("plain_turned", 7, lambda t: plain[t // 2][:, t % 2, :])
-        scaled0 = [sb(f"scaled0{u}", [P, P, 2], F32) for u in range(2)]
-        for u in range(2):
-            nc.scalar.activation(scaled0[u][:], h_turned0[:, 2 * u : 2 * u + 2, :].rearrange("j e p -> j p e"), COPY, scale=share_col[:, 0:1])
+        scaled0 = sb("scaled0", [P, 2, P, 2], F32)
+        nc.scalar.activation(scaled0[:], h_turned0[:].rearrange("j (u e) p -> j u p e", e=2), COPY, scale=share_col[:, 0:1])
         late = sb("late", [P, PACK, P], F32, tag="late_identity")
         for t in range(PACK):
             nc.scalar.activation(late[:, t, :], partners(t, 3 * P, P), COPY)
-        own[3] = staged("own3", [P, PACK, P], F32, 2048)
+        own[3] = staged("own3", [P, PACK, P], F32, 3072)
         for t in range(PACK):
             nc.gpsimd.tensor_tensor(own[3][:, t, :], h_sb[t][:, 3 * P : S], lam_rows[:, P : 2 * P], MULT)
 
         def mix(b, tag=None):
-            z = staged("z1", [P, P, PACK], BF16, 0) if b == 1 else sb(f"z{b}", [P, P, PACK], BF16, tag=tag)
+            z = staged("z1", [P, P, PACK], BF16, 2048) if b == 1 else sb(f"z{b}", [P, P, PACK], BF16, tag=tag)
             nc.vector.tensor_tensor(walk_packed(z[:]), walk(own[b][:]), walk(part[:, :, P * (b - 1) : P * b]), ADD)
             return z
 
+        own[2] = staged("own2", [P, PACK, P], F32, 0)
+        for t, cols, ps in h_ps[1:]:
+            nc.vector.tensor_tensor(own[2][:, t, :], ps[:, HALF - cols.start : 3 * P - cols.start], lam_rows[:, 0:P], MULT)
         z1 = mix(1)
         z0_turned = sb("z0_turned", [P, 2, P, 2], BF16)
         for u in range(2):
@@ -222,13 +224,10 @@ def tile_picked_mixup_none_lo_kernel(tc, xT, w1, w2, lam, mu, offs, pos1, out_0,
                 z0_turned[:, u, :, :],
                 plain_turned[:, 2 * u : 2 * u + 2, :].rearrange("j e p -> j p e"),
                 share_col[:, 2:3],
-                scaled0[u][:],
+                scaled0[:, u, :, :],
                 MULT,
                 ADD,
             )
-        own[2] = sb("own2", [P, PACK, P], F32, tag="scaled00")
-        for t, cols, ps in h_ps[1:]:
-            nc.vector.tensor_tensor(own[2][:, t, :], ps[:, HALF - cols.start : 3 * P - cols.start], lam_rows[:, 0:P], MULT)
         words_ps = bank("words_ps", [P, 2, P], 5)
         z0_words = z0_turned[:].rearrange("j u p e -> j (u p e)").bitcast(F32)
         for u in range(2):
@@ -241,8 +240,8 @@ def tile_picked_mixup_none_lo_kernel(tc, xT, w1, w2, lam, mu, offs, pos1, out_0,
         y_scale_rows = out_2.rearrange("z q c -> q (z c)").bitcast(I32)
         y_scales = sb("y_scales", [P, S], U8)
 
-        def quantise_z(name, z, n):
-            codes = sb(f"{name}_codes", [P, n], U32)
+        def quantise_z(name, z, n, tag=None):
+            codes = sb(f"{name}_codes", [P, n], U32, tag=tag)
             scales = sb(f"{name}_scales", [P, n], U8)
             quantise(codes[:], scales[:], z[:].rearrange("p n t -> p (n t)"))
             return codes, scales
@@ -266,24 +265,36 @@ def tile_picked_mixup_none_lo_kernel(tc, xT, w1, w2, lam, mu, offs, pos1, out_0,
 
         y1 = second_layer(1, quantise_z("z1", z1, P), (6,))
         z2 = mix(2)
-        zq0 = quantise_z("z0", z0, P)
         nc.vector.tensor_tensor(part[:, :, 2 * P : 3 * P], late[:], mu_rows[:, 2 * P : 3 * P].unsqueeze(1).to_broadcast([P, PACK, P]), MULT)
-        y0 = second_layer(0, zq0, (7,))
         y2 = second_layer(2, quantise_z("z2", z2, P), (0,))
-        z3 = mix(3, "z0")
-        y_bf = sb("y_bf", [P, 3 * P, PACK], BF16)
+        y0 = second_layer(0, quantise_z("z0", z0, P, "late_identity"), (7,))
+        z3 = sb("z3", [P, P, PACK], BF16)
+        zq3 = sb("z3_codes", [P, P], U32), sb("z3_scales", [P, P], U8)
+        pieces = [slice(0, M_HALF), slice(M_HALF, P)]
+        for piece in pieces:
+            far = slice(2 * P + piece.start, 2 * P + piece.stop)
+            nc.vector.tensor_tensor(walk_packed(z3[:, piece, :]), walk(own[3][:, :, piece]), walk(part[:, :, far]), ADD)
+        for piece in pieces:
+            quantise(zq3[0][:, piece], zq3[1][:, piece], z3[:, piece, :].rearrange("p n t -> p (n t)"))
+        y3 = sb("y3", [P, PACK, P], F32)
+        y3_bf = sb("y3_bf", [P, P, PACK], BF16)
+        for u in range(2):
+            ps = bank(f"y_ps3{u}", [P, 2, P], 1 + u)
+            for e in range(2):
+                product(ps[:, e, :], w2_codes, w2_scales, 2 * u + e, zq3[0][:], zq3[1][:])
+            nc.scalar.copy(y3[:, 2 * u : 2 * u + 2, :], ps[:])
+            if u == 1:
+                nc.scalar.copy(y3_bf[:, :, 2:PACK], ps[:].rearrange("p e n -> p n e"))
+        nc.sync.dma_start(y_rows[:, :, 3 * P : S], y3[:])
+        y_bf = sb("y_bf", [P, 3 * P, PACK], BF16, tag="part")
         round_y(y_bf[:, P:HALF, :], y1)
-        zq3 = quantise_z("z3", z3, P)
-        y3 = second_layer(3, zq3, (1, 2))
         round_y(y_bf[:, 0:P, :], y0)
         round_y(y_bf[:, HALF : 3 * P, :], y2)
         y_codes = sb("y_codes", [P, 3 * P], U32)
         quantise_y(y_codes[:, 0:HALF], y_bf[:, 0:HALF, :], 0, HALF)
+        nc.vector.tensor_copy(y3_bf[:, :, 0:2], y3[:, 0:2, :].rearrange("p e n -> p n e"))
         quantise_y(y_codes[:, HALF : 3 * P], y_bf[:, HALF : 3 * P, :], HALF, P)
         nc.sync.dma_start(y_words[:, 0 : 3 * P], y_codes[:].bitcast(I32))
-        y3_bf = sb("y3_bf", [P, P, PACK], BF16)
-        for u in range(2):
-            nc.vector.tensor_copy(y3_bf[:, :, 2 * u : 2 * u + 2], y3[:, 2 * u : 2 * u + 2, :].rearrange("p e n -> p n e"))
         y3_codes = sb("y3_codes", [P, P], U32)
         quantise_y(y3_codes[:], y3_bf[:], 3 * P, P)
         nc.sync.dma_start(y_words[:, 3 * P : S], y3_codes[:].bitcast(I32))

@@ -60,7 +60,7 @@ def tile_picked_mixup_none_lo_kernel(tc, xT, w1, w2, lam, mu, offs, pos1, out_0,
         halves = [slice(0, HALF), slice(HALF, S)]
 
         x_plane = [sb(f"x_plane{t}", [P, T], F32) for t in range(PACK)]
-        w1_raw = [sb("w1_raw0", [P, 2, H], F32), staged("w1_raw1", [P, 2, H], F32, 0)]
+        w1_raw = [sb("w1_raw0", [P, 2, H], F32), staged("w1_raw1", [P, 2, H], F32, 2048)]
         mu_rows = sb("mu_rows", [P, 3 * P], F32)
         lam_rows = sb("lam_rows", [P, 2 * P], F32)
 
@@ -150,7 +150,7 @@ def tile_picked_mixup_none_lo_kernel(tc, xT, w1, w2, lam, mu, offs, pos1, out_0,
                 h_ps.append((t, cols, bank(f"h_ps{t}{v}", [P, cols.stop - cols.start], len(h_ps))))
                 product(h_ps[-1][2][:], w1_codes, w1_scales, t, x_codes[:, cols], x_scales[:, cols])
 
-        w2_bf = [staged(f"w2_bf{u}", [P, 2, P, PACK], BF16, 2048 * u) for u in range(2)]
+        w2_bf = [staged(f"w2_bf{u}", [P, 2, P, PACK], BF16, 2048 * (u + 1)) for u in range(2)]
         deal_w2(0)
 
         h_sb = [sb(f"h_sb{t}", [P, S], F32) for t in range(PACK)]
@@ -179,9 +179,9 @@ def tile_picked_mixup_none_lo_kernel(tc, xT, w1, w2, lam, mu, offs, pos1, out_0,
             nc.scalar.activation(scaled[:], h_turned[:], COPY, scale=share_col[:, b : b + 1])
             return turn(f"own{b}", number, lambda t: scaled[:, t, :])
 
-        part = sb("part", [P, PACK, 3 * P], F32)
+        part = sb("part", [P, PACK, HALF], F32)
         for t in range(PACK):
-            nc.vector.tensor_tensor(part[:, t, 0:HALF], partners(t, P, HALF), mu_rows[:, 0:HALF], MULT)
+            nc.vector.tensor_tensor(part[:, t, :], partners(t, P, HALF), mu_rows[:, 0:HALF], MULT)
 
         def gather_plain(name, u, j0, tag):
             plain = sb(name, [P, 2, P], F32, tag=tag)
@@ -200,21 +200,22 @@ def tile_picked_mixup_none_lo_kernel(tc, xT, w1, w2, lam, mu, offs, pos1, out_0,
         own = {1: own_share(1, h_turned1, 0)}
         plain.append(gather_plain("plain1", 1, 0, "late_identity"))
         plain_turned = turn("plain_turned", 7, lambda t: plain[t // 2][:, t % 2, :])
-        scaled0 = sb("scaled0", [P, 2, P, 2], F32)
-        nc.scalar.activation(scaled0[:], h_turned0[:].rearrange("j (u e) p -> j u p e", e=2), COPY, scale=share_col[:, 0:1])
+        scaled0 = [staged("scaled00", [P, P, 2], F32, 7168), sb("scaled01", [P, P, 2], F32)]
+        for u in range(2):
+            nc.scalar.activation(scaled0[u][:], h_turned0[:, 2 * u : 2 * u + 2, :].rearrange("j e p -> j p e"), COPY, scale=share_col[:, 0:1])
         late = sb("late", [P, PACK, P], F32, tag="late_identity")
         for t in range(PACK):
             nc.scalar.activation(late[:, t, :], partners(t, 3 * P, P), COPY)
-        own[3] = staged("own3", [P, PACK, P], F32, 3072)
+        own[3] = staged("own3", [P, PACK, P], F32, 5120)
         for t in range(PACK):
             nc.gpsimd.tensor_tensor(own[3][:, t, :], h_sb[t][:, 3 * P : S], lam_rows[:, P : 2 * P], MULT)
 
-        def mix(b, tag=None):
-            z = staged("z1", [P, P, PACK], BF16, 2048) if b == 1 else sb(f"z{b}", [P, P, PACK], BF16, tag=tag)
+        def mix(b):
+            z = staged(f"z{b}", [P, P, PACK], BF16, (4096, 7680)[b - 1])
             nc.vector.tensor_tensor(walk_packed(z[:]), walk(own[b][:]), walk(part[:, :, P * (b - 1) : P * b]), ADD)
             return z
 
-        own[2] = staged("own2", [P, PACK, P], F32, 0)
+        own[2] = staged("own2", [P, PACK, P], F32, 1024)
         for t, cols, ps in h_ps[1:]:
             nc.vector.tensor_tensor(own[2][:, t, :], ps[:, HALF - cols.start : 3 * P - cols.start], lam_rows[:, 0:P], MULT)
         z1 = mix(1)
@@ -224,7 +225,7 @@ def tile_picked_mixup_none_lo_kernel(tc, xT, w1, w2, lam, mu, offs, pos1, out_0,
                 z0_turned[:, u, :, :],
                 plain_turned[:, 2 * u : 2 * u + 2, :].rearrange("j e p -> j p e"),
                 share_col[:, 2:3],
-                scaled0[:, u, :, :],
+                scaled0[u][:],
                 MULT,
                 ADD,
             )
@@ -241,7 +242,7 @@ def tile_picked_mixup_none_lo_kernel(tc, xT, w1, w2, lam, mu, offs, pos1, out_0,
         y_scales = sb("y_scales", [P, S], U8)
 
         def quantise_z(name, z, n, tag=None):
-            codes = sb(f"{name}_codes", [P, n], U32, tag=tag)
+            codes = staged("z1_codes", [P, n], U32, 7168) if name == "z1" else sb(f"{name}_codes", [P, n], U32, tag=tag)
             scales = sb(f"{name}_scales", [P, n], U8)
             quantise(codes[:], scales[:], z[:].rearrange("p n t -> p (n t)"))
             return codes, scales
@@ -265,15 +266,15 @@ def tile_picked_mixup_none_lo_kernel(tc, xT, w1, w2, lam, mu, offs, pos1, out_0,
 
         y1 = second_layer(1, quantise_z("z1", z1, P), (6,))
         z2 = mix(2)
-        nc.vector.tensor_tensor(part[:, :, 2 * P : 3 * P], late[:], mu_rows[:, 2 * P : 3 * P].unsqueeze(1).to_broadcast([P, PACK, P]), MULT)
+        part3 = staged("part3", [P, PACK, P], F32, 3072)
+        nc.vector.tensor_tensor(part3[:], late[:], mu_rows[:, 2 * P : 3 * P].unsqueeze(1).to_broadcast([P, PACK, P]), MULT)
         y2 = second_layer(2, quantise_z("z2", z2, P), (0,))
         y0 = second_layer(0, quantise_z("z0", z0, P, "late_identity"), (7,))
         z3 = sb("z3", [P, P, PACK], BF16)
         zq3 = sb("z3_codes", [P, P], U32), sb("z3_scales", [P, P], U8)
         pieces = [slice(0, M_HALF), slice(M_HALF, P)]
         for piece in pieces:
-            far = slice(2 * P + piece.start, 2 * P + piece.stop)
-            nc.vector.tensor_tensor(walk_packed(z3[:, piece, :]), walk(own[3][:, :, piece]), walk(part[:, :, far]), ADD)
+            nc.vector.tensor_tensor(walk_packed(z3[:, piece, :]), walk(own[3][:, :, piece]), walk(part3[:, :, piece]), ADD)
         for piece in pieces:
             quantise(zq3[0][:, piece], zq3[1][:, piece], z3[:, piece, :].rearrange("p n t -> p (n t)"))
         y3 = sb("y3", [P, PACK, P], F32)
@@ -286,7 +287,7 @@ def tile_picked_mixup_none_lo_kernel(tc, xT, w1, w2, lam, mu, offs, pos1, out_0,
             if u == 1:
                 nc.scalar.copy(y3_bf[:, :, 2:PACK], ps[:].rearrange("p e n -> p n e"))
         nc.sync.dma_start(y_rows[:, :, 3 * P : S], y3[:])
-        y_bf = sb("y_bf", [P, 3 * P, PACK], BF16, tag="part")
+        y_bf = staged("y_bf", [P, 3 * P, PACK], BF16, 3072)
         round_y(y_bf[:, P:HALF, :], y1)
         round_y(y_bf[:, 0:P, :], y0)
         round_y(y_bf[:, HALF : 3 * P, :], y2)

from contextlib import ExitStack

import concourse.mybir as mybir
from concourse.masks import make_identity

K, T, S, H = 512, 1024, 512, 512
FLOPS = 2 * K * H * S + 2 * H * H * S

F32 = mybir.dt.float32
BF16 = mybir.dt.bfloat16
I32 = mybir.dt.int32
U32 = mybir.dt.uint32
U16 = mybir.dt.uint16
U8 = mybir.dt.uint8
FP8X4 = mybir.dt.float8_e4m3fn_x4
MULT = mybir.AluOpType.mult
ADD = mybir.AluOpType.add
COPY = mybir.ActivationFunctionType.Copy

P = 128
PACK = 4
RUN = 4
HALF = S // 2
M_HALF = P // 2


def tile_picked_mixup_none_lo_kernel(tc, xT, w1, w2, lam, mu, offs, pos1, out_0, out_1, out_2):
    nc = tc.nc
    with ExitStack() as ctx:
        keep = ctx.enter_context(tc.tile_pool(name="keep", bufs=1))
        stage = ctx.enter_context(tc.tile_pool(name="stage", bufs=1))
        psum = ctx.enter_context(tc.psum_pool(name="psum", bufs=1))

        def sb(name, shape, dtype, tag=None):
            return keep.tile(shape, dtype, name=name, tag=tag or name, align_bytes=64)

        def staged(name, shape, dtype, offset):
            return stage.tile(shape, dtype, name=name, offset=offset, align_bytes=64)

        def bank(name, shape, number):
            return psum.tile(shape, F32, name=name, tag=f"bank{number}")

        offs_sb = keep.tile([P, S // 16], U16, name="offs_sb")
        pos_sb = keep.tile([P, S // 16], U16, name="pos_sb")
        zero = sb("zero", [P, 1], F32)
        nc.gpsimd.memset(zero[:], 0.0)
        share_rows = sb("share_rows", [P, P], F32)
        nc.gpsimd.memset(share_rows[:], 0.0)
        nc.scalar.dma_start(share_rows[0:2, :], lam[0:1, 0 : 2 * P].rearrange("r (b m) -> (r b) m", m=P))
        nc.scalar.dma_start(share_rows[2:3, :], mu[0:1, 0:P])
        identity = sb("identity", [P, P], F32)
        nc.scalar.copy(identity[:], zero[:].to_broadcast([P, P]))
        make_identity(nc, identity[:], nomemset=True)
        late_identity = sb("late_identity", [P, P], F32)
        make_identity(nc, late_identity[:])

        x_rows = xT.rearrange("(p t) n -> p t n", t=PACK)
        w1_rows = w1.rearrange("(p j) c -> p j c", j=PACK)
        w2_rows = w2.rearrange("(p j) c -> p j c", j=PACK)
        halves = [slice(0, HALF), slice(HALF, S)]

        x_plane = [sb(f"x_plane{t}", [P, T], F32) for t in range(PACK)]
        w1_raw = [sb("w1_raw0", [P, 2, H], F32), staged("w1_raw1", [P, 2, H], F32, 2048)]
        mu_rows = sb("mu_rows", [P, 3 * P], F32)
        lam_rows = sb("lam_rows", [P, 2 * P], F32)

        nc.sync.dma_start(x_plane[0][:], x_rows[:, 0, :])
        nc.sync.dma_start(offs_sb[:], offs)
        for t in range(1, PACK):
            nc.sync.dma_start(x_plane[t][:], x_rows[:, t, :])
        for v in range(2):
            nc.sync.dma_start(w1_raw[v][:], w1_rows[:, 2 * v : 2 * v + 2, :])
        w2_raw = [sb("w2_raw0", [P, PACK, HALF], F32)]
        nc.sync.dma_start(w2_raw[0][:], w2_rows[:, :, halves[0]])
        nc.sync.dma_start(pos_sb[:], pos1)
        nc.sync.dma_start(mu_rows[:], mu[:, P:S])
        w2_raw.append(sb("w2_raw1", [P, PACK, HALF], F32))
        nc.sync.dma_start(w2_raw[1][:], w2_rows[:, :, halves[1]])
        nc.sync.dma_start(lam_rows[:], lam[:, 2 * P : S])

        def quantise(codes, scales, values):
            nc.vector.quantize_mx(codes.bitcast(FP8X4), scales, values)

        def product(out, w_codes, w_scales, t, codes, scales):
            cols = slice(P * t, P * (t + 1))
            nc.tensor.matmul_mx(
                out=out,
                lhsT=w_codes[:, cols].bitcast(FP8X4),
                lhsT_scale=w_scales[:, cols],
                rhs=codes.bitcast(FP8X4),
                rhs_scale=scales,
                start=True,
                stop=True,
            )

        def deal_w2(v):
            for u in range(2):
                nc.vector.tensor_copy(
                    w2_bf[u][:, :, M_HALF * v : M_HALF * (v + 1), :].rearrange("p t m j -> p m j t"),
                    w2_raw[v][:].rearrange("p j (m t) -> p m j t", t=PACK)[:, :, :, 2 * u : 2 * u + 2],
                )

        def walk(ap):
            return ap.rearrange("p t (g i) -> p g t i", i=RUN)

        def walk_packed(ap):
            return ap.rearrange("p (g i) t -> p g t i", i=RUN)

        x_bf = sb("x_bf", [P, S, PACK], BF16)
        x_codes = sb("x_codes", [P, S], U32)
        x_scales = sb("x_scales", [P, S], U8)

        def gather_plane(pair, t):
            nc.vector.tensor_copy(pair[0][:, t % 2, :], x_plane[t][:].indirect(offs_sb[:, 0 : HALF // 16]))
            nc.scalar.activation(pair[1][:, t % 2, :], x_plane[t][:].indirect(offs_sb[:, HALF // 16 : S // 16]), COPY)

        pair0 = [sb(f"pair0{u}", [P, 2, HALF], F32, tag=f"x_pair0{u}") for u in range(2)]
        gather_plane(pair0, 0)
        gather_plane(pair0, 1)
        for u, half in enumerate(halves):
            nc.vector.tensor_copy(x_bf[:, half, 0:2], pair0[u][:].rearrange("p e n -> p n e"))
        pair1 = [sb("pair10", [P, 2, HALF], F32, tag="x_pair00"), sb("pair11", [P, 2, HALF], F32, tag="x_pair11")]
        gather_plane(pair1, 2)
        gather_plane(pair1, 3)
        for u, half in enumerate(halves):
            nc.vector.tensor_copy(x_bf[:, half, 2:4], pair1[u][:].rearrange("p e n -> p n e"))
        w1_pair = [sb("w1_pair0", [P, 2, P, PACK], BF16, tag="x_plane3"), sb("w1_pair1", [P, 2, P, PACK], BF16, tag="x_pair00")]

        def deal_w1(copy, u, v):
            copy(
                w1_pair[u][:, :, :, 2 * v : 2 * v + 2].rearrange("p t m j -> p m j t"),
                w1_raw[v][:].rearrange("p j (m t) -> p m j t", t=PACK)[:, :, :, 2 * u : 2 * u + 2],
            )

        deal_w1(nc.scalar.copy, 0, 0)
        deal_w1(nc.scalar.copy, 1, 0)
        for half in halves:
            quantise(x_codes[:, half], x_scales[:, half], x_bf[:, half, :].rearrange("p n t -> p (n t)"))
        for t in range(2):
            nc.vector.tensor_copy(w1_pair[0][:, t, :, 2:PACK], w1_raw[1][:].rearrange("p j (m t) -> p t m j", t=PACK)[:, t, :, :])
        deal_w1(nc.scalar.copy, 1, 1)

        w1_codes = sb("w1_codes", [P, H], U32)
        w1_scales = sb("w1_scales", [P, H], U8)
        h_ps = []
        for t in range(PACK):
            tile_cols = slice(P * t, P * (t + 1))
            quantise(w1_codes[:, tile_cols], w1_scales[:, tile_cols], w1_pair[t // 2][:, t % 2, :, :].rearrange("p m j -> p (m j)"))
            for v, cols in enumerate(halves if t == 0 else [slice(0, S)]):
                h_ps.append((t, cols, bank(f"h_ps{t}{v}", [P, cols.stop - cols.start], len(h_ps))))
                product(h_ps[-1][2][:], w1_codes, w1_scales, t, x_codes[:, cols], x_scales[:, cols])

        w2_bf = [staged(f"w2_bf{u}", [P, 2, P, PACK], BF16, 2048 * (u + 1)) for u in range(2)]
        deal_w2(0)

        h_sb = [sb(f"h_sb{t}", [P, S], F32) for t in range(PACK)]
        for t, cols, ps in h_ps[:4]:
            nc.scalar.copy(h_sb[t][:, cols], ps[:])
        share_ps = bank("share_ps", [P, P], 7)
        share_col = sb("share_col", [P, 3], F32)
        nc.tensor.transpose(share_ps[:], share_rows[:], identity[:])
        nc.scalar.copy(h_sb[3][:], h_ps[4][2][:])
        nc.scalar.copy(share_col[:], share_ps[:, 0:3])

        def partners(t, j0, n):
            return h_sb[t][:].indirect(pos_sb[:, j0 // 16 : (j0 + n) // 16])

        def turn(name, number, src, last=identity):
            turned = bank(name, [P, PACK, P], number)
            for t in range(PACK):
                nc.tensor.transpose(turned[:, t, :], src(t), (last if t == PACK - 1 else identity)[:])
            return turned

        def turn_h(b, number, last=identity):
            return turn(f"h_turned{b}", number, lambda t: h_sb[t][:, P * b : P * (b + 1)], last)

        def own_share(b, h_turned, number):
            scaled = sb(f"scaled{b}", [P, PACK, P], F32)
            nc.scalar.activation(scaled[:], h_turned[:], COPY, scale=share_col[:, b : b + 1])
            return turn(f"own{b}", number, lambda t: scaled[:, t, :])

        part = sb("part", [P, PACK, HALF], F32)
        for t in range(PACK):
            nc.vector.tensor_tensor(part[:, t, :], partners(t, P, HALF), mu_rows[:, 0:HALF], MULT)

        def gather_plain(name, u, j0, tag):
            plain = sb(name, [P, 2, P], F32, tag=tag)
            for e in range(2):
                nc.scalar.activation(plain[:, e, :], partners(2 * u + e, j0, P), COPY)
            return plain

        plain = [gather_plain("plain0", 0, 0, "x_codes")]
        h_turned1 = turn_h(1, 5)
        h_turned0 = turn_h(0, 6, late_identity)
        deal_w2(1)
        w2_codes = sb("w2_codes", [P, H], U32)
        w2_scales = sb("w2_scales", [P, H], U8)
        for u in range(2):
            quantise(w2_codes[:, halves[u]], w2_scales[:, halves[u]], w2_bf[u][:].rearrange("p t m j -> p (t m j)"))
        own = {1: own_share(1, h_turned1, 0)}
        plain.append(gather_plain("plain1", 1, 0, "late_identity"))
        plain_turned = turn("plain_turned", 7, lambda t: plain[t // 2][:, t % 2, :])
        scaled0 = [staged("scaled00", [P, P, 2], F32, 7168), sb("scaled01", [P, P, 2], F32)]
        for u in range(2):
            nc.scalar.activation(scaled0[u][:], h_turned0[:, 2 * u : 2 * u + 2, :].rearrange("j e p -> j p e"), COPY, scale=share_col[:, 0:1])
        late = sb("late", [P, PACK, P], F32, tag="late_identity")
        for t in range(PACK):
            nc.scalar.activation(late[:, t, :], partners(t, 3 * P, P), COPY)
        own[3] = staged("own3", [P, PACK, P], F32, 5120)
        for t in range(PACK):
            nc.gpsimd.tensor_tensor(own[3][:, t, :], h_sb[t][:, 3 * P : S], lam_rows[:, P : 2 * P], MULT)

        def mix(b):
            z = staged(f"z{b}", [P, P, PACK], BF16, (4096, 7680)[b - 1])
            nc.vector.tensor_tensor(walk_packed(z[:]), walk(own[b][:]), walk(part[:, :, P * (b - 1) : P * b]), ADD)
            return z

        own[2] = staged("own2", [P, PACK, P], F32, 1024)
        for t, cols, ps in h_ps[1:]:
            nc.vector.tensor_tensor(own[2][:, t, :], ps[:, HALF - cols.start : 3 * P - cols.start], lam_rows[:, 0:P], MULT)
        z1 = mix(1)
        z0_turned = sb("z0_turned", [P, 2, P, 2], BF16)
        for u in range(2):
            nc.vector.scalar_tensor_tensor(
                z0_turned[:, u, :, :],
                plain_turned[:, 2 * u : 2 * u + 2, :].rearrange("j e p -> j p e"),
                share_col[:, 2:3],
                scaled0[u][:],
                MULT,
                ADD,
            )
        words_ps = bank("words_ps", [P, 2, P], 5)
        z0_words = z0_turned[:].rearrange("j u p e -> j (u p e)").bitcast(F32)
        for u in range(2):
            nc.tensor.transpose(words_ps[:, u, :], z0_words[:, P * u : P * (u + 1)], identity[:])
        z0 = sb("z0", [P, P, PACK], BF16)
        nc.scalar.copy(z0[:].rearrange("p n t -> p (n t)").bitcast(F32).rearrange("p (n u) -> p n u", u=2), words_ps[:].rearrange("p u n -> p n u"))

        y_rows = out_0.rearrange("(p t) n -> p t n", t=PACK)
        y_words = out_1.rearrange("z p c r -> p (z c r)").bitcast(I32)
        y_scale_rows = out_2.rearrange("z q c -> q (z c)").bitcast(I32)
        y_scales = sb("y_scales", [P, S], U8)

        def quantise_z(name, z, n, tag=None):
            codes = staged("z1_codes", [P, n], U32, 7168) if name == "z1" else sb(f"{name}_codes", [P, n], U32, tag=tag)
            scales = sb(f"{name}_scales", [P, n], U8)
            quantise(codes[:], scales[:], z[:].rearrange("p n t -> p (n t)"))
            return codes, scales

        def second_layer(b, zq, numbers):
            y = sb(f"y{b}", [P, PACK, P], F32)
            per = PACK // len(numbers)
            for u, number in enumerate(numbers):
                ps = bank(f"y_ps{b}{u}", [P, per, P], number)
                for e in range(per):
                    product(ps[:, e, :], w2_codes, w2_scales, per * u + e, zq[0][:], zq[1][:])
                nc.scalar.copy(y[:, per * u : per * (u + 1), :], ps[:])
            nc.sync.dma_start(y_rows[:, :, P * b : P * (b + 1)], y[:])
            return y

        def round_y(y_bf, y):
            nc.vector.tensor_copy(walk_packed(y_bf), walk(y[:]))

        def quantise_y(codes, y_bf, j0, n):
            quantise(codes, y_scales[:, j0 : j0 + n], y_bf.rearrange("p n t -> p (n t)"))

        y1 = second_layer(1, quantise_z("z1", z1, P), (6,))
        z2 = mix(2)
        part3 = staged("part3", [P, PACK, P], F32, 3072)
        nc.vector.tensor_tensor(part3[:], late[:], mu_rows[:, 2 * P : 3 * P].unsqueeze(1).to_broadcast([P, PACK, P]), MULT)
        y2 = second_layer(2, quantise_z("z2", z2, P), (0,))
        y0 = second_layer(0, quantise_z("z0", z0, P, "late_identity"), (7,))
        z3 = sb("z3", [P, P, PACK], BF16)
        zq3 = sb("z3_codes", [P, P], U32), sb("z3_scales", [P, P], U8)
        pieces = [slice(0, M_HALF), slice(M_HALF, P)]
        for piece in pieces:
            nc.vector.tensor_tensor(walk_packed(z3[:, piece, :]), walk(own[3][:, :, piece]), walk(part3[:, :, piece]), ADD)
        for piece in pieces:
            quantise(zq3[0][:, piece], zq3[1][:, piece], z3[:, piece, :].rearrange("p n t -> p (n t)"))
        y3 = sb("y3", [P, PACK, P], F32)
        y3_bf = sb("y3_bf", [P, P, PACK], BF16)
        for u in range(2):
            ps = bank(f"y_ps3{u}", [P, 2, P], 1 + u)
            for e in range(2):
                product(ps[:, e, :], w2_codes, w2_scales, 2 * u + e, zq3[0][:], zq3[1][:])
            nc.scalar.copy(y3[:, 2 * u : 2 * u + 2, :], ps[:])
            if u == 1:
                nc.scalar.copy(y3_bf[:, :, 2:PACK], ps[:].rearrange("p e n -> p n e"))
        nc.sync.dma_start(y_rows[:, :, 3 * P : S], y3[:])
        y_bf = staged("y_bf", [P, 3 * P, PACK], BF16, 3072)
        round_y(y_bf[:, P:HALF, :], y1)
        round_y(y_bf[:, 0:P, :], y0)
        round_y(y_bf[:, HALF : 3 * P, :], y2)
        y_codes = sb("y_codes", [P, 3 * P], U32)
        quantise_y(y_codes[:, 0:HALF], y_bf[:, 0:HALF, :], 0, HALF)
        nc.vector.tensor_copy(y3_bf[:, :, 0:2], y3[:, 0:2, :].rearrange("p e n -> p n e"))
        quantise_y(y_codes[:, HALF : 3 * P], y_bf[:, HALF : 3 * P, :], HALF, P)
        nc.sync.dma_start(y_words[:, 0 : 3 * P], y_codes[:].bitcast(I32))
        y3_codes = sb("y3_codes", [P, P], U32)
        quantise_y(y3_codes[:], y3_bf[:], 3 * P, P)
        nc.sync.dma_start(y_words[:, 3 * P : S], y3_codes[:].bitcast(I32))
        for q in range(4):
            nc.sync.dma_start(y_scale_rows[4 * q : 4 * q + 4, :], y_scales[32 * q : 32 * q + 4, :].bitcast(I32))
